import numpy as np
import ml_dtypes


def mxq(x, axis, fmt="e4m3"):
    dtype, down = {"e4m3": (ml_dtypes.float8_e4m3fn, 7), "e5m2": (ml_dtypes.float8_e5m2, 14)}[fmt]
    v = np.moveaxis(np.asarray(x, np.float32).astype(ml_dtypes.bfloat16).astype(np.float64), axis, -1)
    blocks = v.reshape(v.shape[:-1] + (-1, 32))
    amax = np.abs(blocks).max(-1, keepdims=True)
    byte = np.maximum(np.where(amax > 0, np.frexp(amax)[1] - 1 + 127, 0) - down, 1)
    scale = np.exp2(byte - 127.0)
    codes = (blocks / scale).astype(np.float32).astype(dtype).astype(np.float64)
    return np.moveaxis((codes * scale).reshape(v.shape), -1, axis)


WIDE = False


def mx_kscale(k):
    if not WIDE:
        return np.ones(k)
    levels = np.array([10, -10, 5, -5, 0])
    if k % 512:
        return np.exp2(np.random.permutation(np.resize(levels, k // 32))).repeat(32)
    a = np.empty((k // 512, 16))
    for p in range(k // 512):
        a[p, :8] = np.random.permutation(np.resize(levels, 8))
        for g in range(8):
            far = levels[np.abs(levels - a[p, g]) >= 10]
            a[p, g + 8] = far[np.random.randint(len(far))]
    return np.exp2(a.ravel()).repeat(32)


BF16 = ml_dtypes.bfloat16


def bf(x):
    return np.asarray(x, np.float32).astype(BF16)


def f64(x):
    return np.asarray(x).astype(np.float64)

def planes(Y):
    n, m = Y.shape
    b = f64(bf(Y)).reshape(n // 32, 32, m)
    amax = np.abs(b).max(1)
    byte = np.clip(np.where(amax > 0, np.frexp(amax)[1] - 1 + 127 - 7, 1), 1, 254)
    codes = (b * np.exp2(127.0 - byte)[:, None, :]).reshape(n, m).astype(np.float32).astype(ml_dtypes.float8_e4m3fn).view(np.uint8)
    words = codes.reshape(n // 512, 128, 4, m).transpose(0, 1, 3, 2)
    return np.ascontiguousarray(words), np.ascontiguousarray(byte.astype(np.uint8).reshape(n // 512, 16, m))


B, S, D, F = 2, 1024, 512, 1536
GELU_C = np.sqrt(2.0 / np.pi)
GELU_A = 0.044715

def setup_inputs():
    s = mx_kscale(D)
    t = mx_kscale(S)
    spread = np.exp(0.8 * np.random.randn(F))
    x = np.random.randn(B, S, D) * s
    w1 = np.random.randn(D, F) * spread / np.sqrt(D) / s[:, None]
    b1 = 0.3 * np.random.randn(F) * spread
    tok = (1.0 + 0.1 * np.random.randn(S)) * t
    w2 = np.random.randn(S, S) / np.sqrt(S) / t[:, None]
    res = 0.7 * np.random.randn(B, S, F) * spread
    return {"x": bf(x), "w1": bf(w1), "b1": bf(b1), "tok": bf(tok),
            "w2": bf(w2), "res": bf(res)}

def reference(x, w1, b1, tok, w2, res):
    x, w1, b1, tok, w2, res = f64(x), f64(w1), f64(b1), f64(tok), f64(w2), f64(res)
    z = (mxq(x, 2, "e4m3") @ mxq(w1, 0, "e4m3")) + b1
    a = 0.5 * z * (1.0 + np.tanh(GELU_C * (z + GELU_A * z * z * z)))
    h = a * tok[:, None]
    mix = mxq(w2, 0, "e4m3").T @ mxq(h, 1, "e4m3")
    y = mix + res
    Y = y.reshape(B * S, F).T
    words, scales = planes(Y)
    return y, words, scales

@@ -1,0 +1,338 @@
+from contextlib import ExitStack
+
+import concourse.mybir as mybir
+from concourse.masks import make_identity
+
+B, S, D, F = 2, 1024, 512, 1536
+FLOPS = 2 * B * S * D * F + 2 * B * S * S * F
+
+F32 = mybir.dt.float32
+BF16 = mybir.dt.bfloat16
+I32 = mybir.dt.int32
+U32 = mybir.dt.uint32
+U8 = mybir.dt.uint8
+FP8X4 = mybir.dt.float8_e4m3fn_x4
+GELU = mybir.ActivationFunctionType.Gelu_apprx_tanh
+ADD = mybir.AluOpType.add
+MULT = mybir.AluOpType.mult
+
+P = 128
+PACK = 4
+GROUP = P * PACK
+PIECE = 256
+F_GROUPS = F // GROUP
+S_GROUPS = S // GROUP
+STEPS_PER_UNIT = 4
+UNITS = B * F_GROUPS
+STEPS = UNITS * STEPS_PER_UNIT
+LAG = 6
+
+
+def tile_gelu_token_mix_residual_h3_kernel(tc, x, w1, b1, tok, w2, res, out_0, out_1, out_2):
+    nc = tc.nc
+    with ExitStack() as ctx:
+        sb = ctx.enter_context(tc.tile_pool(name="sb", bufs=1))
+        ps = ctx.enter_context(tc.psum_pool(name="ps", bufs=1))
+        ctx.enter_context(tc.manual_schedule())
+
+        def tiles(name, count, shape, dtype):
+            return [sb.tile(shape, dtype, name="%s%d" % (name, i), align_bytes=64) for i in range(count)]
+
+        def banks(name, count):
+            return [ps.tile([P, GROUP], F32, name="%s%d" % (name, i)) for i in range(count)]
+
+        z_bank = banks("z_bank", 2)
+        a_bank = banks("a_bank", 2)
+        mix_bank = banks("mix_bank", 2)
+        y_bank, x_bank = banks("word_bank", 2)
+
+        ident = sb.tile([P, P], F32, name="ident", align_bytes=64)
+        b_raw = sb.tile([F // P, P], BF16, name="b_raw", align_bytes=64)
+        b_rows = sb.tile([P, P], F32, name="b_rows", align_bytes=64)
+        b_cols = sb.tile([P, F // P], F32, name="b_cols", align_bytes=64)
+        tok_sb = sb.tile([P, S_GROUPS, PACK], BF16, name="tok_sb", align_bytes=64)
+
+        x_raw = tiles("x_raw", B * S_GROUPS * 2, [P, 2, D], BF16)
+        w1_raw = tiles("w1_raw", F_GROUPS, [P, PACK, GROUP], BF16)
+        w2_raw = tiles("w2_raw", S_GROUPS, [P, PACK, S], BF16)
+        res_sb = tiles("res_sb", 3, [P, S // P, GROUP], BF16)
+        w_packed = tiles("w_packed", 4, [P, PIECE, PACK], BF16)
+        x_packed = tiles("x_packed", 2, [P, 2 * PIECE], F32)
+        x_codes = tiles("x_codes", B * S_GROUPS, [P, GROUP], U32)
+        x_scales = tiles("x_scales", B * S_GROUPS, [P, GROUP], U8)
+        w1_codes = tiles("w1_codes", F_GROUPS, [P, GROUP], U32)
+        w1_scales = tiles("w1_scales", F_GROUPS, [P, GROUP], U8)
+        w2_codes = tiles("w2_codes", S_GROUPS, [P, S], U32)
+        w2_scales = tiles("w2_scales", S_GROUPS, [P, S], U8)
+        act = tiles("act", 6, [P, GROUP], F32)
+        h_packed = tiles("h_packed", 3, [P, PIECE, PACK], BF16)
+        h_codes = tiles("h_codes", 3 * S_GROUPS, [P, GROUP], U32)
+        h_scales = tiles("h_scales", 3 * S_GROUPS, [P, GROUP], U8)
+        y_sb = tiles("y_sb", 4, [P, 2, GROUP], F32)
+        y_round = tiles("y_round", 3, [P, 2, 2 * P, 2], BF16)
+        y_packed = tiles("y_packed", 3, [P, 2 * PIECE], F32)
+        y_codes = tiles("y_codes", 2, [P, S], U32)
+        y_scales = tiles("y_scales", 2, [P, S], U8)
+
+        def quantize(codes, scales, piece, packed):
+            cols = slice(piece * PIECE, (piece + 1) * PIECE)
+            nc.vector.quantize_mx(out=codes[:, cols].bitcast(FP8X4), scales=scales[:, cols], in_=packed)
+
+        def matmul(bank, l_codes, l_scales, l_tile, r_codes, r_scales, start, stop):
+            cols = slice(l_tile * P, (l_tile + 1) * P)
+            nc.tensor.matmul_mx(
+                out=bank[:],
+                lhsT=l_codes[:, cols].bitcast(FP8X4),
+                lhsT_scale=l_scales[:, cols],
+                rhs=r_codes[:].bitcast(FP8X4),
+                rhs_scale=r_scales[:],
+                start=start,
+                stop=stop,
+            )
+
+        def load_x(xg, half):
+            b, g = divmod(xg, S_GROUPS)
+            rows = x[b, g * GROUP : (g + 1) * GROUP, :].rearrange("(p t) d -> p t d", t=PACK)
+            nc.sync.dma_start(out=x_raw[2 * xg + half][:], in_=rows[:, 2 * half : 2 * half + 2, :])
+
+        def load_w1(fg):
+            cols = w1[:, fg * GROUP : (fg + 1) * GROUP]
+            nc.sync.dma_start(out=w1_raw[fg][:], in_=cols.rearrange("(p t) c -> p t c", t=PACK))
+
+        def load_w2(g):
+            rows = w2[g * GROUP : (g + 1) * GROUP, :]
+            nc.sync.dma_start(out=w2_raw[g][:], in_=rows.rearrange("(p t) c -> p t c", t=PACK))
+
+        def load_res(unit):
+            b, fg = divmod(unit, F_GROUPS)
+            cols = res[b, :, fg * GROUP : (fg + 1) * GROUP]
+            nc.sync.dma_start(out=res_sb[unit % 3][:], in_=cols.rearrange("(a j) f -> j a f", j=P))
+
+        def w_parts(wp):
+            if wp < 2 * F_GROUPS:
+                fg, piece = divmod(wp, 2)
+                return w1_raw[fg], w1_codes[fg], w1_scales[fg], piece
+            piece, g = divmod(wp - 2 * F_GROUPS, S_GROUPS)
+            return w2_raw[g], w2_codes[g], w2_scales[g], piece
+
+        slot_of = {}
+
+        def pack_w(wp, on_vector):
+            raw, codes, scales, piece = w_parts(wp)
+            slot_of[wp] = len(slot_of) % 4
+            dst = w_packed[slot_of[wp]][:].rearrange("p (c i) t -> p c t i", i=4)
+            src = raw[:, :, piece * PIECE : (piece + 1) * PIECE].rearrange("p t (c i) -> p c t i", i=4)
+            if on_vector:
+                nc.vector.tensor_copy(out=dst, in_=src)
+            else:
+                nc.scalar.copy(out=dst, in_=src)
+
+        def quantize_w(wp):
+            raw, codes, scales, piece = w_parts(wp)
+            quantize(codes, scales, piece, w_packed[slot_of[wp]][:].rearrange("p c t -> p (c t)"))
+
+        def word_view(bank):
+            return bank[:].rearrange("p (a u j) -> p a u j", a=2, u=2)
+
+        def copy_words(dst, bank, on_vector):
+            out = dst[:].rearrange("p (a j u) -> p a j u", a=2, u=2)
+            in_ = bank[:].rearrange("p (a u j) -> p a j u", a=2, u=2)
+            if on_vector:
+                nc.vector.tensor_copy(out=out, in_=in_)
+            else:
+                nc.scalar.copy(out=out, in_=in_)
+
+        def turn_x(xh, bank):
+            for a in range(2):
+                words = x_raw[xh][:, a, :].bitcast(F32)
+                for u in range(2):
+                    nc.tensor.transpose(word_view(bank)[:, a, u, :], words[:, u : D // 2 : 2], ident[:])
+
+        def quantize_x(xh):
+            quantize(x_codes[xh // 2], x_scales[xh // 2], xh % 2, x_packed[xh % 2][:].bitcast(BF16))
+
+        def first(step):
+            unit, d = divmod(step, STEPS_PER_UNIT)
+            b, fg = divmod(unit, F_GROUPS)
+            g, piece = divmod(d, 2)
+            return unit, b, fg, g, piece
+
+        def z_matmul(step, i):
+            unit, b, fg, g, piece = first(step)
+            xg = b * S_GROUPS + g
+            matmul(z_bank[i], w1_codes[fg], w1_scales[fg], 2 * piece + i, x_codes[xg], x_scales[xg], True, True)
+
+        def gelu(step, i):
+            unit, b, fg, g, piece = first(step)
+            ft = PACK * fg + 2 * piece + i
+            nc.scalar.activation(out=act[2 * (step % 3) + i][:], in_=z_bank[i][:], func=GELU, bias=b_cols[:, ft : ft + 1])
+
+        def turn_act(step, i):
+            for t in range(PACK):
+                cols = slice(t * P, (t + 1) * P)
+                nc.tensor.transpose(a_bank[i][:, cols], act[2 * (step % 3) + i][:, cols], ident[:])
+
+        def scale_tokens(step, i):
+            unit, b, fg, g, piece = first(step)
+            nc.vector.tensor_tensor(
+                out=h_packed[step % 3][:, i * P : (i + 1) * P, :],
+                in0=a_bank[i][:].rearrange("p (t f) -> p f t", t=PACK),
+                in1=tok_sb[:, g, :].unsqueeze(1).to_broadcast([P, P, PACK]),
+                op=MULT,
+            )
+
+        def quantize_h(step):
+            unit, b, fg, g, piece = first(step)
+            hg = (unit % 3) * S_GROUPS + g
+            quantize(h_codes[hg], h_scales[hg], piece, h_packed[step % 3][:].rearrange("p c t -> p (c t)"))
+
+        def mix_matmul(step, i):
+            unit, piece = divmod(step, STEPS_PER_UNIT)
+            for g in range(S_GROUPS):
+                hg = (unit % 3) * S_GROUPS + g
+                matmul(
+                    mix_bank[i], w2_codes[g], w2_scales[g], 2 * piece + i, h_codes[hg], h_scales[hg],
+                    g == 0, g == S_GROUPS - 1,
+                )
+
+        def add_res(step, i):
+            unit, piece = divmod(step, STEPS_PER_UNIT)
+            nc.vector.tensor_tensor(
+                out=y_sb[step % 4][:, i, :], in0=mix_bank[i][:], in1=res_sb[unit % 3][:, 2 * piece + i, :], op=ADD
+            )
+
+        def store_y(step):
+            unit, piece = divmod(step, STEPS_PER_UNIT)
+            b, fg = divmod(unit, F_GROUPS)
+            dst = out_0[b, piece * PIECE : (piece + 1) * PIECE, fg * GROUP : (fg + 1) * GROUP]
+            nc.sync.dma_start(out=dst.rearrange("(a j) f -> j a f", j=P), in_=y_sb[step % 4][:])
+
+        def round_y(step):
+            nc.scalar.copy(
+                out=y_round[step % 3][:],
+                in_=y_sb[step % 4][:].rearrange("j a f -> j (a f)").rearrange("j (q u e) -> j u q e", u=2, e=2),
+            )
+
+        def turn_y(step):
+            words = y_round[step % 3][:].rearrange("j u q e -> j (u q e)").bitcast(F32)
+            for a in range(2):
+                for u in range(2):
+                    start = (2 * u + a) * P
+                    nc.tensor.transpose(word_view(y_bank)[:, a, u, :], words[:, start : start + P], ident[:])
+
+        def quantize_y(step):
+            unit, piece = divmod(step, STEPS_PER_UNIT)
+            quantize(y_codes[unit % 2], y_scales[unit % 2], piece, y_packed[step % 3][:].bitcast(BF16))
+
+        def store_planes(step):
+            unit, piece = divmod(step, STEPS_PER_UNIT)
+            b, fg = divmod(unit, F_GROUPS)
+            if piece % 2 == 1:
+                lo = (piece - 1) * PIECE
+                words = out_1[fg].rearrange("p m t -> p (m t)").bitcast(I32)
+                nc.sync.dma_start(
+                    out=words[:, b * S + lo : b * S + lo + 2 * PIECE],
+                    in_=y_codes[unit % 2][:, lo : lo + 2 * PIECE].bitcast(I32),
+                )
+            if piece == STEPS_PER_UNIT - 1:
+                rows = out_2[fg].bitcast(I32)
+                for q in range(4):
+                    nc.sync.dma_start(
+                        out=rows[4 * q : 4 * q + 4, b * S // 4 : (b + 1) * S // 4],
+                        in_=y_scales[unit % 2][32 * q : 32 * q + 4, :].bitcast(I32),
+                    )
+
+        load_x(0, 0)
+        load_x(0, 1)
+        load_w1(0)
+        nc.sync.dma_start(out=b_raw[:], in_=b1.rearrange("(r c) -> r c", c=P))
+        nc.sync.dma_start(out=tok_sb[:], in_=tok.rearrange("(g p t) -> p g t", g=S_GROUPS, t=PACK))
+        load_x(1, 0)
+        load_x(1, 1)
+        load_w2(0)
+        load_w2(1)
+        load_w1(1)
+        load_res(0)
+        load_w1(2)
+        for xh in range(4, 8):
+            load_x(xh // 2, xh % 2)
+
+        make_identity(nc, ident[:])
+        nc.scalar.activation(out=b_rows[:], in_=ident[:], func=GELU)
+
+        turn_x(0, x_bank)
+        turn_x(1, y_bank)
+        copy_words(x_packed[0], x_bank, False)
+        copy_words(x_packed[1], y_bank, False)
+        nc.scalar.copy(out=b_rows[0 : F // P, :], in_=b_raw[:])
+        nc.tensor.transpose(mix_bank[0][:, 0:P], b_rows[:], ident[:])
+        quantize_x(0)
+        pack_w(0, True)
+        quantize_x(1)
+        quantize_w(0)
+        nc.vector.tensor_copy(out=b_cols[:], in_=mix_bank[0][:, 0 : F // P])
+        pack_w(1, True)
+
+        vector_packs = {1: [6], 2: [2], 3: [3], 4: [7], 5: [11], 6: [4], 7: [5]}
+        scalar_packs = {1: [8], 2: [10], 3: [12], 4: [9], 5: [13]}
+        x_half_at = {8: 4, 9: 5, 10: 6, 11: 7}
+
+        for n in range(STEPS + LAG + 3):
+            c = n - LAG
+            has_z = n < STEPS
+            has_mix = 0 <= c < STEPS
+            to_quantize = ([1] if n == 0 else []) + vector_packs.get(n - 1, []) + scalar_packs.get(n - 1, [])
+            if n % STEPS_PER_UNIT == 1 and 1 <= n // STEPS_PER_UNIT < UNITS:
+                load_res(n // STEPS_PER_UNIT)
+            if 0 <= c - 1 < STEPS:
+                round_y(c - 1)
+            for i in range(2):
+                if has_mix:
+                    mix_matmul(c, i)
+            for i in range(2):
+                if has_z:
+                    z_matmul(n, i)
+            if has_mix:
+                add_res(c, 0)
+            for wp in to_quantize:
+                quantize_w(wp)
+            if 0 <= n - 2 < STEPS:
+                quantize_h(n - 2)
+            if has_mix:
+                add_res(c, 1)
+                store_y(c)
+            if 0 <= c - 2 < STEPS:
+                quantize_y(c - 2)
+                store_planes(c - 2)
+            if n == 1:
+                quantize_x(2)
+                quantize_x(3)
+            if n - 1 in x_half_at:
+                quantize_x(x_half_at[n - 1])
+            for wp in vector_packs.get(n, []):
+                pack_w(wp, True)
+            for i in range(2):
+                if has_z:
+                    gelu(n, i)
+            if n == 0:
+                turn_x(2, x_bank)
+                turn_x(3, y_bank)
+                copy_words(x_packed[0], x_bank, True)
+                copy_words(x_packed[1], y_bank, True)
+            if 0 <= n - 1 < STEPS:
+                turn_act(n - 1, 0)
+            if 0 <= c - 1 < STEPS:
+                turn_y(c - 1)
+            if 0 <= n - 1 < STEPS:
+                turn_act(n - 1, 1)
+            if n in x_half_at:
+                turn_x(x_half_at[n], x_bank)
+            for i in range(2):
+                if 0 <= n - 1 < STEPS:
+                    scale_tokens(n - 1, i)
+            if 0 <= c - 1 < STEPS:
+                copy_words(y_packed[(c - 1) % 3], y_bank, False)
+            if n in x_half_at:
+                copy_words(x_packed[x_half_at[n] % 2], x_bank, False)
+            for wp in scalar_packs.get(n, []):
+                pack_w(wp, False)

@@ -44,7 +44,7 @@ def tile_gelu_token_mix_residual_h3_kernel(tc, x, w1, b1, tok, w2, res, out_0, o
         z_bank = banks("z_bank", 2)
         a_bank = banks("a_bank", 2)
         mix_bank = banks("mix_bank", 2)
-        y_bank, x_bank = banks("word_bank", 2)
+        word_bank = banks("word_bank", 2)
 
         ident = sb.tile([P, P], F32, name="ident", align_bytes=64)
         b_raw = sb.tile([F // P, P], BF16, name="b_raw", align_bytes=64)
@@ -54,10 +54,10 @@ def tile_gelu_token_mix_residual_h3_kernel(tc, x, w1, b1, tok, w2, res, out_0, o
 
         x_raw = tiles("x_raw", B * S_GROUPS * 2, [P, 2, D], BF16)
         w1_raw = tiles("w1_raw", F_GROUPS, [P, PACK, GROUP], BF16)
-        w2_raw = tiles("w2_raw", S_GROUPS, [P, PACK, S], BF16)
+        w2_raw = tiles("w2_raw", 2 * S_GROUPS, [P, PACK, GROUP], BF16)
         res_sb = tiles("res_sb", 3, [P, S // P, GROUP], BF16)
-        w_packed = tiles("w_packed", 4, [P, PIECE, PACK], BF16)
-        x_packed = tiles("x_packed", 2, [P, 2 * PIECE], F32)
+        w_packed = tiles("w_packed", 5, [P, PIECE, PACK], BF16)
+        x_packed = tiles("x_packed", 4, [P, 2 * PIECE], F32)
         x_codes = tiles("x_codes", B * S_GROUPS, [P, GROUP], U32)
         x_scales = tiles("x_scales", B * S_GROUPS, [P, GROUP], U8)
         w1_codes = tiles("w1_codes", F_GROUPS, [P, GROUP], U32)
@@ -69,7 +69,7 @@ def tile_gelu_token_mix_residual_h3_kernel(tc, x, w1, b1, tok, w2, res, out_0, o
         h_codes = tiles("h_codes", 3 * S_GROUPS, [P, GROUP], U32)
         h_scales = tiles("h_scales", 3 * S_GROUPS, [P, GROUP], U8)
         y_sb = tiles("y_sb", 4, [P, 2, GROUP], F32)
-        y_round = tiles("y_round", 3, [P, 2, 2 * P, 2], BF16)
+        y_round = tiles("y_round", 3, [P, 2, 2, P, 2], BF16)
         y_packed = tiles("y_packed", 3, [P, 2 * PIECE], F32)
         y_codes = tiles("y_codes", 2, [P, S], U32)
         y_scales = tiles("y_scales", 2, [P, S], U8)
@@ -99,12 +99,12 @@ def tile_gelu_token_mix_residual_h3_kernel(tc, x, w1, b1, tok, w2, res, out_0, o
             cols = w1[:, fg * GROUP : (fg + 1) * GROUP]
             nc.sync.dma_start(out=w1_raw[fg][:], in_=cols.rearrange("(p t) c -> p t c", t=PACK))
 
-        def load_w2(g):
-            rows = w2[g * GROUP : (g + 1) * GROUP, :]
-            nc.sync.dma_start(out=w2_raw[g][:], in_=rows.rearrange("(p t) c -> p t c", t=PACK))
+        def load_w2(half, g):
+            rows = w2[g * GROUP : (g + 1) * GROUP, half * GROUP : (half + 1) * GROUP]
+            nc.sync.dma_start(out=w2_raw[2 * g + half][:], in_=rows.rearrange("(p t) c -> p t c", t=PACK))
 
         def load_res(unit):
-            b, fg = divmod(unit, F_GROUPS)
+            fg, b = divmod(unit, B)
             cols = res[b, :, fg * GROUP : (fg + 1) * GROUP]
             nc.sync.dma_start(out=res_sb[unit % 3][:], in_=cols.rearrange("(a j) f -> j a f", j=P))
 
@@ -113,23 +113,30 @@ def tile_gelu_token_mix_residual_h3_kernel(tc, x, w1, b1, tok, w2, res, out_0, o
                 fg, piece = divmod(wp, 2)
                 return w1_raw[fg], w1_codes[fg], w1_scales[fg], piece
             piece, g = divmod(wp - 2 * F_GROUPS, S_GROUPS)
-            return w2_raw[g], w2_codes[g], w2_scales[g], piece
+            return w2_raw[2 * g + piece // 2], w2_codes[g], w2_scales[g], piece
 
-        slot_of = {}
+        chain = [(6, 0, 256), (7, 0, 256), (9, 0, 256), (11, 0, 256), (12, 0, 256), (13, 0, 256), (2, 0, 256), (3, 0, 256), (4, 0, 256), (5, 0, 256)]
+        slot_of = dict([(wp, 4 if wp in [item[0] for item in chain] else wp % 4) for wp in range(14)])
 
-        def pack_w(wp, on_vector):
+        def pack_w(wp, engine, lo=0, hi=PIECE):
             raw, codes, scales, piece = w_parts(wp)
-            slot_of[wp] = len(slot_of) % 4
-            dst = w_packed[slot_of[wp]][:].rearrange("p (c i) t -> p c t i", i=4)
-            src = raw[:, :, piece * PIECE : (piece + 1) * PIECE].rearrange("p t (c i) -> p c t i", i=4)
-            if on_vector:
+            base = (piece % 2) * PIECE
+            dst = w_packed[slot_of[wp]][:, 0 : hi - lo, :].rearrange("p (c i) t -> p c t i", i=4)
+            src = raw[:, :, base + lo : base + hi].rearrange("p t (c i) -> p c t i", i=4)
+            if engine == "vector":
                 nc.vector.tensor_copy(out=dst, in_=src)
-            else:
+            elif engine == "scalar":
                 nc.scalar.copy(out=dst, in_=src)
+            else:
+                dst = w_packed[slot_of[wp]][:, 0 : hi - lo, :]
+                src = raw[:, :, base + lo : base + hi].rearrange("p t c -> p c t")
+                nc.gpsimd.tensor_scalar(out=dst, in0=src, scalar1=1.0, scalar2=0.0, op0=MULT, op1=ADD)
 
-        def quantize_w(wp):
+        def quantize_w(wp, lo=0, hi=PIECE):
             raw, codes, scales, piece = w_parts(wp)
-            quantize(codes, scales, piece, w_packed[slot_of[wp]][:].rearrange("p c t -> p (c t)"))
+            cols = slice(piece * PIECE + lo, piece * PIECE + hi)
+            packed = w_packed[slot_of[wp]][:, 0 : hi - lo, :].rearrange("p c t -> p (c t)")
+            nc.vector.quantize_mx(out=codes[:, cols].bitcast(FP8X4), scales=scales[:, cols], in_=packed)
 
         def word_view(bank):
             return bank[:].rearrange("p (a u j) -> p a u j", a=2, u=2)
@@ -149,23 +156,30 @@ def tile_gelu_token_mix_residual_h3_kernel(tc, x, w1, b1, tok, w2, res, out_0, o
                     nc.tensor.transpose(word_view(bank)[:, a, u, :], words[:, u : D // 2 : 2], ident[:])
 
         def quantize_x(xh):
-            quantize(x_codes[xh // 2], x_scales[xh // 2], xh % 2, x_packed[xh % 2][:].bitcast(BF16))
+            quantize(x_codes[xh // 2], x_scales[xh // 2], xh % 2, x_packed[xh % 4][:].bitcast(BF16))
 
         def first(step):
             unit, d = divmod(step, STEPS_PER_UNIT)
-            b, fg = divmod(unit, F_GROUPS)
+            fg, b = divmod(unit, B)
             g, piece = divmod(d, 2)
             return unit, b, fg, g, piece
+
+        def z_of(step, i):
+            return mix_bank[i] if step < LAG and step % 2 == 1 else z_bank[i]
+
+        def mix_of(step, i):
+            return z_bank[i] if step > STEPS - LAG and step % 2 == 1 else mix_bank[i]
 
         def z_matmul(step, i):
             unit, b, fg, g, piece = first(step)
             xg = b * S_GROUPS + g
-            matmul(z_bank[i], w1_codes[fg], w1_scales[fg], 2 * piece + i, x_codes[xg], x_scales[xg], True, True)
+            for again in range(2 if (2 <= step < LAG and i < 0) else 1):
+                matmul(z_of(step, i), w1_codes[fg], w1_scales[fg], 2 * piece + i, x_codes[xg], x_scales[xg], True, True)
 
         def gelu(step, i):
             unit, b, fg, g, piece = first(step)
             ft = PACK * fg + 2 * piece + i
-            nc.scalar.activation(out=act[2 * (step % 3) + i][:], in_=z_bank[i][:], func=GELU, bias=b_cols[:, ft : ft + 1])
+            nc.scalar.activation(out=act[2 * (step % 3) + i][:], in_=z_of(step, i)[:], func=GELU, bias=b_cols[:, ft : ft + 1])
 
         def turn_act(step, i):
             for t in range(PACK):
@@ -191,34 +205,36 @@ def tile_gelu_token_mix_residual_h3_kernel(tc, x, w1, b1, tok, w2, res, out_0, o
             for g in range(S_GROUPS):
                 hg = (unit % 3) * S_GROUPS + g
                 matmul(
-                    mix_bank[i], w2_codes[g], w2_scales[g], 2 * piece + i, h_codes[hg], h_scales[hg],
+                    mix_of(step, i), w2_codes[g], w2_scales[g], 2 * piece + i, h_codes[hg], h_scales[hg],
                     g == 0, g == S_GROUPS - 1,
                 )
 
         def add_res(step, i):
             unit, piece = divmod(step, STEPS_PER_UNIT)
             nc.vector.tensor_tensor(
-                out=y_sb[step % 4][:, i, :], in0=mix_bank[i][:], in1=res_sb[unit % 3][:, 2 * piece + i, :], op=ADD
+                out=y_sb[step % 4][:, i, :], in0=mix_of(step, i)[:], in1=res_sb[unit % 3][:, 2 * piece + i, :], op=ADD
             )
 
         def store_y(step):
             unit, piece = divmod(step, STEPS_PER_UNIT)
-            b, fg = divmod(unit, F_GROUPS)
+            fg, b = divmod(unit, B)
             dst = out_0[b, piece * PIECE : (piece + 1) * PIECE, fg * GROUP : (fg + 1) * GROUP]
             nc.sync.dma_start(out=dst.rearrange("(a j) f -> j a f", j=P), in_=y_sb[step % 4][:])
 
-        def round_y(step):
-            nc.scalar.copy(
-                out=y_round[step % 3][:],
-                in_=y_sb[step % 4][:].rearrange("j a f -> j (a f)").rearrange("j (q u e) -> j u q e", u=2, e=2),
-            )
+        def round_y(step, lo, hi, on_vector):
+            out = y_round[step % 3][:, lo:hi, :, :, :]
+            in_ = y_sb[step % 4][:, lo:hi, :].rearrange("j a (p u e) -> j a u p e", u=2, e=2)
+            if on_vector:
+                nc.vector.tensor_copy(out=out, in_=in_)
+            else:
+                nc.scalar.copy(out=out, in_=in_)
 
         def turn_y(step):
-            words = y_round[step % 3][:].rearrange("j u q e -> j (u q e)").bitcast(F32)
+            words = y_round[step % 3][:].rearrange("j a u p e -> j (a u p e)").bitcast(F32)
             for a in range(2):
                 for u in range(2):
-                    start = (2 * u + a) * P
-                    nc.tensor.transpose(word_view(y_bank)[:, a, u, :], words[:, start : start + P], ident[:])
+                    start = (2 * a + u) * P
+                    nc.tensor.transpose(word_view(word_bank[step % 2])[:, a, u, :], words[:, start : start + P], ident[:])
 
         def quantize_y(step):
             unit, piece = divmod(step, STEPS_PER_UNIT)
@@ -226,113 +242,171 @@ def tile_gelu_token_mix_residual_h3_kernel(tc, x, w1, b1, tok, w2, res, out_0, o
 
         def store_planes(step):
             unit, piece = divmod(step, STEPS_PER_UNIT)
-            b, fg = divmod(unit, F_GROUPS)
-            if piece % 2 == 1:
-                lo = (piece - 1) * PIECE
+            fg, b = divmod(unit, B)
+            count = 1 if step >= STEPS - 2 else 2
+            if count == 1 or piece % 2 == 1:
+                lo, hi = (piece + 1 - count) * PIECE, (piece + 1) * PIECE
                 words = out_1[fg].rearrange("p m t -> p (m t)").bitcast(I32)
-                nc.sync.dma_start(
-                    out=words[:, b * S + lo : b * S + lo + 2 * PIECE],
-                    in_=y_codes[unit % 2][:, lo : lo + 2 * PIECE].bitcast(I32),
-                )
+                nc.sync.dma_start(out=words[:, b * S + lo : b * S + hi], in_=y_codes[unit % 2][:, lo:hi].bitcast(I32))
             if piece == STEPS_PER_UNIT - 1:
                 rows = out_2[fg].bitcast(I32)
                 for q in range(4):
-                    nc.sync.dma_start(
+                    queue = nc.scalar if unit == UNITS - 1 and q % 2 == 1 else nc.sync
+                    queue.dma_start(
                         out=rows[4 * q : 4 * q + 4, b * S // 4 : (b + 1) * S // 4],
                         in_=y_scales[unit % 2][32 * q : 32 * q + 4, :].bitcast(I32),
                     )
 
         load_x(0, 0)
         load_x(0, 1)
-        load_w1(0)
         nc.sync.dma_start(out=b_raw[:], in_=b1.rearrange("(r c) -> r c", c=P))
+        load_w1(0)
         nc.sync.dma_start(out=tok_sb[:], in_=tok.rearrange("(g p t) -> p g t", g=S_GROUPS, t=PACK))
         load_x(1, 0)
         load_x(1, 1)
-        load_w2(0)
-        load_w2(1)
-        load_w1(1)
+        load_w2(0, 0)
+        load_w2(0, 1)
+        load_x(2, 0)
+        load_x(2, 1)
+        load_w2(1, 0)
+        load_w2(1, 1)
+        load_x(3, 0)
+        load_x(3, 1)
         load_res(0)
+        load_w1(1)
+        load_res(1)
         load_w1(2)
-        for xh in range(4, 8):
-            load_x(xh // 2, xh % 2)
 
         make_identity(nc, ident[:])
         nc.scalar.activation(out=b_rows[:], in_=ident[:], func=GELU)
 
-        turn_x(0, x_bank)
-        turn_x(1, y_bank)
-        copy_words(x_packed[0], x_bank, False)
-        copy_words(x_packed[1], y_bank, False)
+        turn_x(0, word_bank[0])
+        turn_x(1, word_bank[1])
+        copy_words(x_packed[0], word_bank[0], False)
         nc.scalar.copy(out=b_rows[0 : F // P, :], in_=b_raw[:])
-        nc.tensor.transpose(mix_bank[0][:, 0:P], b_rows[:], ident[:])
+        copy_words(x_packed[1], word_bank[1], False)
+        nc.tensor.transpose(a_bank[0][:, 0:P], b_rows[:], ident[:])
+        turn_x(2, word_bank[0])
+        copy_words(x_packed[2], word_bank[0], False)
+        if 0 == 0:
+            turn_x(3, word_bank[1])
+            copy_words(x_packed[3], word_bank[1], False)
+        pack_w(0, "vector")
         quantize_x(0)
-        pack_w(0, True)
-        quantize_x(1)
         quantize_w(0)
-        nc.vector.tensor_copy(out=b_cols[:], in_=mix_bank[0][:, 0 : F // P])
-        pack_w(1, True)
+        quantize_x(1)
+        nc.vector.tensor_copy(out=b_cols[:], in_=a_bank[0][:, 0 : F // P])
+        pack_w(1, "vector")
+        for i in range(2):
+            z_matmul(0, i)
+        quantize_w(1)
 
-        vector_packs = {1: [6], 2: [2], 3: [3], 4: [7], 5: [11], 6: [4], 7: [5]}
-        scalar_packs = {1: [8], 2: [10], 3: [12], 4: [9], 5: [13]}
-        x_half_at = {8: 4, 9: 5, 10: 6, 11: 7}
+        vector_packs = {0: [6]}
+        scalar_packs = {1: [8], 3: [10]}
+        x_half_at = {1: 4, 2: 5, 3: 6, 4: 7}
 
-        for n in range(STEPS + LAG + 3):
+        def live(step):
+            return 0 <= step < STEPS
+
+        def mix_at(n):
             c = n - LAG
-            has_z = n < STEPS
-            has_mix = 0 <= c < STEPS
-            to_quantize = ([1] if n == 0 else []) + vector_packs.get(n - 1, []) + scalar_packs.get(n - 1, [])
-            if n % STEPS_PER_UNIT == 1 and 1 <= n // STEPS_PER_UNIT < UNITS:
+            if c < 30:
+                return [c] if live(c) else []
+            if c == 30:
+                return [c, c + 1]
+            return [c + 1] if c + 1 < STEPS else []
+
+        def finish_tile(a):
+            step = STEPS - 1
+            unit, piece = divmod(step, STEPS_PER_UNIT)
+            bank = a_bank[a]
+            words = y_round[step % 3][:].rearrange("j a u p e -> j (a u p e)").bitcast(F32)
+            for u in range(2):
+                start = (2 * a + u) * P
+                nc.tensor.transpose(bank[:, u * P : (u + 1) * P], words[:, start : start + P], ident[:])
+            packed = y_packed[step % 3][:, a * PIECE : (a + 1) * PIECE]
+            out = packed.rearrange("p (j u) -> p j u", u=2)
+            in_ = bank[:, 0 : 2 * P].rearrange("p (u j) -> p j u", u=2)
+            if a == 0:
+                nc.scalar.copy(out=out, in_=in_)
+            else:
+                nc.vector.tensor_copy(out=out, in_=in_)
+
+        for n in range(STEPS + LAG + 1):
+            c = n - LAG
+            if n % STEPS_PER_UNIT == 1 and 2 <= n // STEPS_PER_UNIT < UNITS:
                 load_res(n // STEPS_PER_UNIT)
-            if 0 <= c - 1 < STEPS:
-                round_y(c - 1)
+            if n >= 40 and live(c - 2):
+                turn_y(c - 2)
+                copy_words(y_packed[(c - 2) % 3], word_bank[c % 2], False)
+            if live(c - 1) and c - 1 < 22:
+                round_y(c - 1, 0, 2, False)
+            for early in mix_at(n):
+                for i in range(2):
+                    mix_matmul(early, i)
             for i in range(2):
-                if has_mix:
-                    mix_matmul(c, i)
-            for i in range(2):
-                if has_z:
+                if live(n) and n >= 2:
                     z_matmul(n, i)
-            if has_mix:
+                if n == 0:
+                    z_matmul(1, i)
+            if live(c):
                 add_res(c, 0)
-            for wp in to_quantize:
-                quantize_w(wp)
-            if 0 <= n - 2 < STEPS:
-                quantize_h(n - 2)
-            if has_mix:
+                if n >= 11 and live(n - 2):
+                    quantize_h(n - 2)
+                if c >= 22:
+                    round_y(c, 0, 1, False)
                 add_res(c, 1)
                 store_y(c)
-            if 0 <= c - 2 < STEPS:
-                quantize_y(c - 2)
-                store_planes(c - 2)
-            if n == 1:
-                quantize_x(2)
-                quantize_x(3)
-            if n - 1 in x_half_at:
-                quantize_x(x_half_at[n - 1])
-            for wp in vector_packs.get(n, []):
-                pack_w(wp, True)
-            for i in range(2):
-                if has_z:
-                    gelu(n, i)
+            for wp in vector_packs.get(n - 1, []):
+                if slot_of[wp] != 4:
+                    quantize_w(wp)
             if n == 0:
-                turn_x(2, x_bank)
-                turn_x(3, y_bank)
-                copy_words(x_packed[0], x_bank, True)
-                copy_words(x_packed[1], y_bank, True)
-            if 0 <= n - 1 < STEPS:
+                quantize_x(2)
+            if n == 0:
+                quantize_x(3)
+            for xh in dict({2: [4], 3: [5], 4: [6], 5: [7]}).get(n, []):
+                quantize_x(xh)
+            if live(n - 2) and n < 11:
+                quantize_h(n - 2)
+            if live(c - 3):
+                quantize_y(c - 3)
+                store_planes(c - 3)
+            for wp in scalar_packs.get(n - 2, []):
+                quantize_w(wp)
+            if live(c) and c >= 22:
+                round_y(c, 1, 2, True)
+            for wp in vector_packs.get(n, []):
+                pack_w(wp, "vector")
+            if 0 <= n - 1 < len(chain):
+                quantize_w(*chain[n - 1])
+            if 1 <= n < len(chain):
+                pack_w(chain[n][0], "gpsimd", chain[n][1], chain[n][2])
+            for i in range(2):
+                if live(n):
+                    gelu(n, i)
+            if n == 0 and 0 == 1:
+                turn_x(3, word_bank[1])
+                copy_words(x_packed[3], word_bank[1], True)
+            if live(n - 1):
                 turn_act(n - 1, 0)
-            if 0 <= c - 1 < STEPS:
-                turn_y(c - 1)
-            if 0 <= n - 1 < STEPS:
+            if live(c - 2) and n < 40:
+                turn_y(c - 2)
+            if live(n - 1):
                 turn_act(n - 1, 1)
             if n in x_half_at:
-                turn_x(x_half_at[n], x_bank)
+                turn_x(x_half_at[n], word_bank[n % 2])
             for i in range(2):
-                if 0 <= n - 1 < STEPS:
+                if live(n - 1):
                     scale_tokens(n - 1, i)
-            if 0 <= c - 1 < STEPS:
-                copy_words(y_packed[(c - 1) % 3], y_bank, False)
+            if live(c - 2) and n < 40:
+                copy_words(y_packed[(c - 2) % 3], word_bank[c % 2], False)
             if n in x_half_at:
-                copy_words(x_packed[x_half_at[n] % 2], x_bank, False)
+                copy_words(x_packed[x_half_at[n] % 4], word_bank[n % 2], False)
             for wp in scalar_packs.get(n, []):
-                pack_w(wp, False)
+                pack_w(wp, "scalar")
+        finish_tile(0)
+        quantize_y(STEPS - 2)
+        store_planes(STEPS - 2)
+        finish_tile(1)
+        quantize_y(STEPS - 1)
+        store_planes(STEPS - 1)

@@ -115,7 +115,7 @@ def tile_gelu_token_mix_residual_h3_kernel(tc, x, w1, b1, tok, w2, res, out_0, o
             piece, g = divmod(wp - 2 * F_GROUPS, S_GROUPS)
             return w2_raw[2 * g + piece // 2], w2_codes[g], w2_scales[g], piece
 
-        chain = [(6, 0, 256), (7, 0, 256), (9, 0, 256), (11, 0, 256), (12, 0, 256), (13, 0, 256), (2, 0, 256), (3, 0, 256), (4, 0, 256), (5, 0, 256)]
+        chain = [(11, 0, 256), (2, 0, 128), (2, 128, 256), (3, 0, 128), (3, 128, 256), (4, 0, 128), (4, 128, 256), (5, 0, 128), (5, 128, 256)]
         slot_of = dict([(wp, 4 if wp in [item[0] for item in chain] else wp % 4) for wp in range(14)])
 
         def pack_w(wp, engine, lo=0, hi=PIECE):
@@ -301,8 +301,8 @@ def tile_gelu_token_mix_residual_h3_kernel(tc, x, w1, b1, tok, w2, res, out_0, o
             z_matmul(0, i)
         quantize_w(1)
 
-        vector_packs = {0: [6]}
-        scalar_packs = {1: [8], 3: [10]}
+        vector_packs = {0: [6], 1: [7], 2: [9], 3: [11]}
+        scalar_packs = {1: [8], 3: [10], 5: [12], 6: [13]}
         x_half_at = {1: 4, 2: 5, 3: 6, 4: 7}
 
         def live(step):
@@ -351,7 +351,7 @@ def tile_gelu_token_mix_residual_h3_kernel(tc, x, w1, b1, tok, w2, res, out_0, o
                     z_matmul(1, i)
             if live(c):
                 add_res(c, 0)
-                if n >= 11 and live(n - 2):
+                if n >= 14 and live(n - 2):
                     quantize_h(n - 2)
                 if c >= 22:
                     round_y(c, 0, 1, False)
@@ -366,7 +366,7 @@ def tile_gelu_token_mix_residual_h3_kernel(tc, x, w1, b1, tok, w2, res, out_0, o
                 quantize_x(3)
             for xh in dict({2: [4], 3: [5], 4: [6], 5: [7]}).get(n, []):
                 quantize_x(xh)
-            if live(n - 2) and n < 11:
+            if live(n - 2) and n < 14:
                 quantize_h(n - 2)
             if live(c - 3):
                 quantize_y(c - 3)
@@ -377,10 +377,10 @@ def tile_gelu_token_mix_residual_h3_kernel(tc, x, w1, b1, tok, w2, res, out_0, o
                 round_y(c, 1, 2, True)
             for wp in vector_packs.get(n, []):
                 pack_w(wp, "vector")
-            if 0 <= n - 1 < len(chain):
-                quantize_w(*chain[n - 1])
-            if 1 <= n < len(chain):
-                pack_w(chain[n][0], "gpsimd", chain[n][1], chain[n][2])
+            if 0 <= n - 4 < len(chain):
+                quantize_w(*chain[n - 4])
+            if 0 <= n - 4 < len(chain) - 1:
+                pack_w(chain[n - 4 + 1][0], "gpsimd", chain[n - 4 + 1][1], chain[n - 4 + 1][2])
             for i in range(2):
                 if live(n):
                     gelu(n, i)

@@ -19,63 +19,94 @@ MULT = mybir.AluOpType.mult
 P = 128
 PACK = 4
 GROUP = P * PACK
-PIECE = 256
+PIECE = 2 * P
+HALF = PIECE // 2
 F_GROUPS = F // GROUP
 S_GROUPS = S // GROUP
+F_TILES = F // P
 STEPS_PER_UNIT = 4
-UNITS = B * F_GROUPS
+UNITS = F_GROUPS * B
 STEPS = UNITS * STEPS_PER_UNIT
-LAG = 6
+LAST = STEPS - 1
+LAG = STEPS_PER_UNIT + 2
+
+W1_FIRST_PASS = 4
+W1_HALVES = (F_GROUPS - 1) * GROUP // HALF
+PAIRS_FIRST = W1_FIRST_PASS + W1_HALVES
+SPLIT_ROUND_FIRST = STEPS - 2
+
+RES_TILES = 3
+W_PACKED_TILES = 4
+X_PACKED_TILES = 4
+ACT_STEPS = 3
+H_PACKED_TILES = 5
+H_UNITS = 3
+Y_TILES = 4
+Y_STAGE_TILES = 3
+PLANE_UNITS = 2
 
 
 def tile_gelu_token_mix_residual_h3_kernel(tc, x, w1, b1, tok, w2, res, out_0, out_1, out_2):
     nc = tc.nc
     with ExitStack() as ctx:
-        sb = ctx.enter_context(tc.tile_pool(name="sb", bufs=1))
-        ps = ctx.enter_context(tc.psum_pool(name="ps", bufs=1))
+        sbuf = ctx.enter_context(tc.tile_pool(name="sbuf", bufs=1))
+        psum = ctx.enter_context(tc.psum_pool(name="psum", bufs=1))
         ctx.enter_context(tc.manual_schedule())
 
         def tiles(name, count, shape, dtype):
-            return [sb.tile(shape, dtype, name="%s%d" % (name, i), align_bytes=64) for i in range(count)]
+            return [sbuf.tile(shape, dtype, name="%s%d" % (name, n), align_bytes=64) for n in range(count)]
 
-        def banks(name, count):
-            return [ps.tile([P, GROUP], F32, name="%s%d" % (name, i)) for i in range(count)]
+        def banks(name):
+            return [psum.tile([P, GROUP], F32, name="%s%d" % (name, i)) for i in range(2)]
 
-        z_bank = banks("z_bank", 2)
-        a_bank = banks("a_bank", 2)
-        mix_bank = banks("mix_bank", 2)
-        word_bank = banks("word_bank", 2)
+        z_bank = banks("z_bank")
+        act_bank = banks("act_bank")
+        mix_bank = banks("mix_bank")
+        pair_bank = banks("pair_bank")
 
-        ident = sb.tile([P, P], F32, name="ident", align_bytes=64)
-        b_raw = sb.tile([F // P, P], BF16, name="b_raw", align_bytes=64)
-        b_rows = sb.tile([P, P], F32, name="b_rows", align_bytes=64)
-        b_cols = sb.tile([P, F // P], F32, name="b_cols", align_bytes=64)
-        tok_sb = sb.tile([P, S_GROUPS, PACK], BF16, name="tok_sb", align_bytes=64)
+        ident = sbuf.tile([P, P], F32, name="ident", align_bytes=64)
+        b_raw = sbuf.tile([F_TILES, P], BF16, name="b_raw", align_bytes=64)
+        b_rows = sbuf.tile([P, P], F32, name="b_rows", align_bytes=64)
+        b_cols = sbuf.tile([P, F_TILES], F32, name="b_cols", align_bytes=64)
+        tok_raw = sbuf.tile([P, S_GROUPS, PACK], BF16, name="tok_raw", align_bytes=64)
+        tok_f32 = sbuf.tile([P, S_GROUPS * PACK], F32, name="tok_f32", align_bytes=64)
+        tok_wide = tiles("tok_wide", S_GROUPS, [P, P // 2, PACK, 2], BF16)
+        tok_rows = tiles("tok_rows", S_GROUPS, [P, GROUP], F32)
 
         x_raw = tiles("x_raw", B * S_GROUPS * 2, [P, 2, D], BF16)
         w1_raw = tiles("w1_raw", F_GROUPS, [P, PACK, GROUP], BF16)
-        w2_raw = tiles("w2_raw", 2 * S_GROUPS, [P, PACK, GROUP], BF16)
-        res_sb = tiles("res_sb", 3, [P, S // P, GROUP], BF16)
-        w_packed = tiles("w_packed", 5, [P, PIECE, PACK], BF16)
-        x_packed = tiles("x_packed", 4, [P, 2 * PIECE], F32)
+        w2_raw = tiles("w2_raw", S_GROUPS * 2, [P, PACK, GROUP], BF16)
+        res_sb = tiles("res_sb", RES_TILES, [P, S // P, GROUP], BF16)
+        w_packed = tiles("w_packed", W_PACKED_TILES, [P, PIECE, PACK], BF16)
+        w_handover = sbuf.tile([P, PIECE, PACK], BF16, name="w_handover", align_bytes=64)
+        x_packed = tiles("x_packed", X_PACKED_TILES, [P, 2 * PIECE], F32)
         x_codes = tiles("x_codes", B * S_GROUPS, [P, GROUP], U32)
         x_scales = tiles("x_scales", B * S_GROUPS, [P, GROUP], U8)
         w1_codes = tiles("w1_codes", F_GROUPS, [P, GROUP], U32)
         w1_scales = tiles("w1_scales", F_GROUPS, [P, GROUP], U8)
         w2_codes = tiles("w2_codes", S_GROUPS, [P, S], U32)
         w2_scales = tiles("w2_scales", S_GROUPS, [P, S], U8)
-        act = tiles("act", 6, [P, GROUP], F32)
-        h_packed = tiles("h_packed", 3, [P, PIECE, PACK], BF16)
-        h_codes = tiles("h_codes", 3 * S_GROUPS, [P, GROUP], U32)
-        h_scales = tiles("h_scales", 3 * S_GROUPS, [P, GROUP], U8)
-        y_sb = tiles("y_sb", 4, [P, 2, GROUP], F32)
-        y_round = tiles("y_round", 3, [P, 2, 2, P, 2], BF16)
-        y_packed = tiles("y_packed", 3, [P, 2 * PIECE], F32)
-        y_codes = tiles("y_codes", 2, [P, S], U32)
-        y_scales = tiles("y_scales", 2, [P, S], U8)
+        act = tiles("act", 2 * ACT_STEPS, [P, GROUP], F32)
+        h_packed = tiles("h_packed", H_PACKED_TILES, [P, PIECE, PACK], BF16)
+        h_codes = tiles("h_codes", H_UNITS * S_GROUPS, [P, GROUP], U32)
+        h_scales = tiles("h_scales", H_UNITS * S_GROUPS, [P, GROUP], U8)
+        y_sb = tiles("y_sb", Y_TILES, [P, 2, GROUP], F32)
+        y_round = tiles("y_round", Y_STAGE_TILES, [P, 2, 2, P, 2], BF16)
+        y_packed = tiles("y_packed", Y_STAGE_TILES, [P, 2 * PIECE], F32)
+        y_codes = tiles("y_codes", PLANE_UNITS, [P, S], U32)
+        y_scales = tiles("y_scales", PLANE_UNITS, [P, S], U8)
 
-        def quantize(codes, scales, piece, packed):
-            cols = slice(piece * PIECE, (piece + 1) * PIECE)
+        def copy_on(engine, out, in_):
+            if engine == "vector":
+                nc.vector.tensor_copy(out=out, in_=in_)
+            else:
+                nc.scalar.copy(out=out, in_=in_)
+
+        def flat(packed):
+            return packed.rearrange("p c t -> p (c t)")
+
+        def quantize(codes, scales, first_col, packed):
+            cols = slice(first_col, first_col + packed.shape[1] // PACK)
             nc.vector.quantize_mx(out=codes[:, cols].bitcast(FP8X4), scales=scales[:, cols], in_=packed)
 
         def matmul(bank, l_codes, l_scales, l_tile, r_codes, r_scales, start, stop):
@@ -90,323 +121,340 @@ def tile_gelu_token_mix_residual_h3_kernel(tc, x, w1, b1, tok, w2, res, out_0, o
                 stop=stop,
             )
 
-        def load_x(xg, half):
-            b, g = divmod(xg, S_GROUPS)
+        def transpose_into(bank, quarter, in_):
+            nc.tensor.transpose(bank[:, quarter * P : (quarter + 1) * P], in_, ident[:])
+
+        def pack_pairs(engine, out, bank, row_tiles):
+            in_ = bank[:, 0 : row_tiles * PIECE].rearrange("p (a u j) -> p a j u", a=row_tiles, u=2)
+            copy_on(engine, out.rearrange("p (a j u) -> p a j u", a=row_tiles, u=2), in_)
+
+
+        def load_x(xh):
+            b, g = divmod(xh // 2, S_GROUPS)
             rows = x[b, g * GROUP : (g + 1) * GROUP, :].rearrange("(p t) d -> p t d", t=PACK)
-            nc.sync.dma_start(out=x_raw[2 * xg + half][:], in_=rows[:, 2 * half : 2 * half + 2, :])
+            nc.sync.dma_start(out=x_raw[xh][:], in_=rows[:, 2 * (xh % 2) : 2 * (xh % 2) + 2, :])
 
         def load_w1(fg):
             cols = w1[:, fg * GROUP : (fg + 1) * GROUP]
             nc.sync.dma_start(out=w1_raw[fg][:], in_=cols.rearrange("(p t) c -> p t c", t=PACK))
 
-        def load_w2(half, g):
-            rows = w2[g * GROUP : (g + 1) * GROUP, half * GROUP : (half + 1) * GROUP]
-            nc.sync.dma_start(out=w2_raw[2 * g + half][:], in_=rows.rearrange("(p t) c -> p t c", t=PACK))
+        def load_w2(g, side):
+            rows = w2[g * GROUP : (g + 1) * GROUP, side * GROUP : (side + 1) * GROUP]
+            nc.sync.dma_start(out=w2_raw[2 * g + side][:], in_=rows.rearrange("(p t) c -> p t c", t=PACK))
 
         def load_res(unit):
             fg, b = divmod(unit, B)
             cols = res[b, :, fg * GROUP : (fg + 1) * GROUP]
-            nc.sync.dma_start(out=res_sb[unit % 3][:], in_=cols.rearrange("(a j) f -> j a f", j=P))
+            nc.sync.dma_start(out=res_sb[unit % RES_TILES][:], in_=cols.rearrange("(a j) f -> j a f", j=P))
 
-        def w_parts(wp):
-            if wp < 2 * F_GROUPS:
-                fg, piece = divmod(wp, 2)
-                return w1_raw[fg], w1_codes[fg], w1_scales[fg], piece
-            piece, g = divmod(wp - 2 * F_GROUPS, S_GROUPS)
-            return w2_raw[2 * g + piece // 2], w2_codes[g], w2_scales[g], piece
 
-        chain = [(11, 0, 256), (2, 0, 128), (2, 128, 256), (3, 0, 128), (3, 128, 256), (4, 0, 128), (4, 128, 256), (5, 0, 128), (5, 128, 256)]
-        slot_of = dict([(wp, 4 if wp in [item[0] for item in chain] else wp % 4) for wp in range(14)])
+        def pack_w(engine, packed, raw, first_col):
+            in_ = raw[:, :, first_col : first_col + PIECE].rearrange("p t (c i) -> p c t i", i=4)
+            copy_on(engine, packed[:].rearrange("p (c i) t -> p c t i", i=4), in_)
 
-        def pack_w(wp, engine, lo=0, hi=PIECE):
-            raw, codes, scales, piece = w_parts(wp)
-            base = (piece % 2) * PIECE
-            dst = w_packed[slot_of[wp]][:, 0 : hi - lo, :].rearrange("p (c i) t -> p c t i", i=4)
-            src = raw[:, :, base + lo : base + hi].rearrange("p t (c i) -> p c t i", i=4)
-            if engine == "vector":
-                nc.vector.tensor_copy(out=dst, in_=src)
-            elif engine == "scalar":
-                nc.scalar.copy(out=dst, in_=src)
-            else:
-                dst = w_packed[slot_of[wp]][:, 0 : hi - lo, :]
-                src = raw[:, :, base + lo : base + hi].rearrange("p t c -> p c t")
-                nc.gpsimd.tensor_scalar(out=dst, in0=src, scalar1=1.0, scalar2=0.0, op0=MULT, op1=ADD)
+        w2_stage = {}
 
-        def quantize_w(wp, lo=0, hi=PIECE):
-            raw, codes, scales, piece = w_parts(wp)
-            cols = slice(piece * PIECE + lo, piece * PIECE + hi)
-            packed = w_packed[slot_of[wp]][:, 0 : hi - lo, :].rearrange("p c t -> p (c t)")
-            nc.vector.quantize_mx(out=codes[:, cols].bitcast(FP8X4), scales=scales[:, cols], in_=packed)
+        def pack_w2(engine, g, piece, packed):
+            w2_stage[(g, piece)] = packed
+            pack_w(engine, packed, w2_raw[2 * g + piece // 2], (piece % 2) * PIECE)
 
-        def word_view(bank):
-            return bank[:].rearrange("p (a u j) -> p a u j", a=2, u=2)
+        def quantize_w2(g, piece):
+            quantize(w2_codes[g], w2_scales[g], piece * PIECE, flat(w2_stage[(g, piece)][:]))
 
-        def copy_words(dst, bank, on_vector):
-            out = dst[:].rearrange("p (a j u) -> p a j u", a=2, u=2)
-            in_ = bank[:].rearrange("p (a u j) -> p a j u", a=2, u=2)
-            if on_vector:
-                nc.vector.tensor_copy(out=out, in_=in_)
-            else:
-                nc.scalar.copy(out=out, in_=in_)
+        def pack_w1_half(half):
+            fg, col = divmod(GROUP + half * HALF, GROUP)
+            in_ = w1_raw[fg][:, :, col : col + HALF].rearrange("p t c -> p c t")
+            nc.gpsimd.tensor_scalar(out=w_handover[:, 0:HALF, :], in0=in_, scalar1=1.0, scalar2=0.0, op0=MULT, op1=ADD)
+
+        def quantize_w1_half(half):
+            fg, col = divmod(GROUP + half * HALF, GROUP)
+            quantize(w1_codes[fg], w1_scales[fg], col, flat(w_handover[:, 0:HALF, :]))
+
 
         def turn_x(xh, bank):
             for a in range(2):
-                words = x_raw[xh][:, a, :].bitcast(F32)
+                pairs = x_raw[xh][:, a, :].bitcast(F32)
                 for u in range(2):
-                    nc.tensor.transpose(word_view(bank)[:, a, u, :], words[:, u : D // 2 : 2], ident[:])
+                    transpose_into(bank, 2 * a + u, pairs[:, u : D // 2 : 2])
+
+        def pack_x(xh, bank):
+            pack_pairs("scalar", x_packed[xh % X_PACKED_TILES][:], bank, 2)
 
         def quantize_x(xh):
-            quantize(x_codes[xh // 2], x_scales[xh // 2], xh % 2, x_packed[xh % 4][:].bitcast(BF16))
+            packed = x_packed[xh % X_PACKED_TILES][:].bitcast(BF16)
+            quantize(x_codes[xh // 2], x_scales[xh // 2], (xh % 2) * PIECE, packed)
 
-        def first(step):
-            unit, d = divmod(step, STEPS_PER_UNIT)
+
+        def widen_tok(g):
+            in_ = tok_raw[:, g, :].unsqueeze(1).unsqueeze(3).to_broadcast([P, P // 2, PACK, 2])
+            nc.scalar.copy(out=tok_wide[g][:], in_=in_)
+
+        def spread_tok(g, bank):
+            for t in range(PACK):
+                transpose_into(bank, t, tok_f32[:, PACK * g + t : PACK * g + t + 1].to_broadcast([P, P]))
+            nc.scalar.copy(
+                out=tok_rows[g][:].rearrange("f (u p e) -> f u p e", u=2, e=2),
+                in_=bank[:].rearrange("f (u e p) -> f u p e", u=2, e=2),
+            )
+
+
+        def first_parts(step):
+            unit, rest = divmod(step, STEPS_PER_UNIT)
             fg, b = divmod(unit, B)
-            g, piece = divmod(d, 2)
-            return unit, b, fg, g, piece
+            g, piece = divmod(rest, 2)
+            return unit, fg, b, g, piece
+
+        def as_pairs(step, i):
+            return i == 1 and PAIRS_FIRST <= step < LAST
+
+        def tile_order(step):
+            return [1, 0] if as_pairs(step, 1) else [0, 1]
 
         def z_of(step, i):
             return mix_bank[i] if step < LAG and step % 2 == 1 else z_bank[i]
 
-        def mix_of(step, i):
-            return z_bank[i] if step > STEPS - LAG and step % 2 == 1 else mix_bank[i]
+        def act_of(step, i):
+            return act[2 * (step % ACT_STEPS) + i]
 
-        def z_matmul(step, i):
-            unit, b, fg, g, piece = first(step)
+        def z_matmuls(step):
+            unit, fg, b, g, piece = first_parts(step)
             xg = b * S_GROUPS + g
-            for again in range(2 if (2 <= step < LAG and i < 0) else 1):
+            for i in tile_order(step):
                 matmul(z_of(step, i), w1_codes[fg], w1_scales[fg], 2 * piece + i, x_codes[xg], x_scales[xg], True, True)
 
         def gelu(step, i):
-            unit, b, fg, g, piece = first(step)
-            ft = PACK * fg + 2 * piece + i
-            nc.scalar.activation(out=act[2 * (step % 3) + i][:], in_=z_of(step, i)[:], func=GELU, bias=b_cols[:, ft : ft + 1])
+            unit, fg, b, g, piece = first_parts(step)
+            f_tile = PACK * fg + 2 * piece + i
+            out, in_ = act_of(step, i)[:], z_of(step, i)[:]
+            if as_pairs(step, i):
+                out = out.rearrange("f (u p e) -> f u p e", u=2, e=2)
+                in_ = in_.rearrange("f (u e p) -> f u p e", u=2, e=2)
+            nc.scalar.activation(out=out, in_=in_, func=GELU, bias=b_cols[:, f_tile : f_tile + 1])
+
+        def h_rows(step):
+            return flat(h_packed[(step - 2) % H_PACKED_TILES][:])[:, 0:GROUP]
+
+        def scale_rows(step):
+            unit, fg, b, g, piece = first_parts(step)
+            nc.gpsimd.tensor_tensor(out=h_rows(step), in0=act_of(step, 1)[:], in1=tok_rows[g][:], op=MULT)
 
         def turn_act(step, i):
-            for t in range(PACK):
-                cols = slice(t * P, (t + 1) * P)
-                nc.tensor.transpose(a_bank[i][:, cols], act[2 * (step % 3) + i][:, cols], ident[:])
+            source = h_rows(step).bitcast(F32) if as_pairs(step, i) else act_of(step, i)[:]
+            for quarter in range(source.shape[1] // P):
+                transpose_into(act_bank[i], quarter, source[:, quarter * P : (quarter + 1) * P])
 
-        def scale_tokens(step, i):
-            unit, b, fg, g, piece = first(step)
-            nc.vector.tensor_tensor(
-                out=h_packed[step % 3][:, i * P : (i + 1) * P, :],
-                in0=a_bank[i][:].rearrange("p (t f) -> p f t", t=PACK),
-                in1=tok_sb[:, g, :].unsqueeze(1).to_broadcast([P, P, PACK]),
-                op=MULT,
-            )
+        def pack_h(step, i):
+            unit, fg, b, g, piece = first_parts(step)
+            packed = h_packed[step % H_PACKED_TILES][:, i * P : (i + 1) * P, :]
+            if as_pairs(step, i):
+                pack_pairs("vector", flat(packed).bitcast(F32), act_bank[i], 1)
+            else:
+                nc.vector.tensor_tensor(
+                    out=packed.rearrange("p (c e) t -> p c t e", e=2),
+                    in0=act_bank[i][:].rearrange("p (t c e) -> p c t e", t=PACK, e=2),
+                    in1=tok_wide[g][:],
+                    op=MULT,
+                )
 
         def quantize_h(step):
-            unit, b, fg, g, piece = first(step)
-            hg = (unit % 3) * S_GROUPS + g
-            quantize(h_codes[hg], h_scales[hg], piece, h_packed[step % 3][:].rearrange("p c t -> p (c t)"))
+            unit, fg, b, g, piece = first_parts(step)
+            hg = (unit % H_UNITS) * S_GROUPS + g
+            quantize(h_codes[hg], h_scales[hg], piece * PIECE, flat(h_packed[step % H_PACKED_TILES][:]))
 
-        def mix_matmul(step, i):
+
+        def mix_of(step, i):
+            return z_bank[i] if step + LAG > STEPS and step % 2 == 1 else mix_bank[i]
+
+        def mix_matmuls(step):
             unit, piece = divmod(step, STEPS_PER_UNIT)
-            for g in range(S_GROUPS):
-                hg = (unit % 3) * S_GROUPS + g
-                matmul(
-                    mix_of(step, i), w2_codes[g], w2_scales[g], 2 * piece + i, h_codes[hg], h_scales[hg],
-                    g == 0, g == S_GROUPS - 1,
-                )
+            for i in range(2):
+                for g in range(S_GROUPS):
+                    hg = (unit % H_UNITS) * S_GROUPS + g
+                    matmul(
+                        mix_of(step, i), w2_codes[g], w2_scales[g], 2 * piece + i, h_codes[hg], h_scales[hg],
+                        g == 0, g == S_GROUPS - 1,
+                    )
 
         def add_res(step, i):
             unit, piece = divmod(step, STEPS_PER_UNIT)
             nc.vector.tensor_tensor(
-                out=y_sb[step % 4][:, i, :], in0=mix_of(step, i)[:], in1=res_sb[unit % 3][:, 2 * piece + i, :], op=ADD
+                out=y_sb[step % Y_TILES][:, i, :],
+                in0=mix_of(step, i)[:],
+                in1=res_sb[unit % RES_TILES][:, 2 * piece + i, :],
+                op=ADD,
             )
 
         def store_y(step):
             unit, piece = divmod(step, STEPS_PER_UNIT)
             fg, b = divmod(unit, B)
-            dst = out_0[b, piece * PIECE : (piece + 1) * PIECE, fg * GROUP : (fg + 1) * GROUP]
-            nc.sync.dma_start(out=dst.rearrange("(a j) f -> j a f", j=P), in_=y_sb[step % 4][:])
+            rows = out_0[b, piece * PIECE : (piece + 1) * PIECE, fg * GROUP : (fg + 1) * GROUP]
+            nc.sync.dma_start(out=rows.rearrange("(a j) f -> j a f", j=P), in_=y_sb[step % Y_TILES][:])
 
-        def round_y(step, lo, hi, on_vector):
-            out = y_round[step % 3][:, lo:hi, :, :, :]
-            in_ = y_sb[step % 4][:, lo:hi, :].rearrange("j a (p u e) -> j a u p e", u=2, e=2)
-            if on_vector:
-                nc.vector.tensor_copy(out=out, in_=in_)
-            else:
-                nc.scalar.copy(out=out, in_=in_)
+        def round_y(engine, step, first_tile, end_tile):
+            in_ = y_sb[step % Y_TILES][:, first_tile:end_tile, :].rearrange("j a (p u e) -> j a u p e", u=2, e=2)
+            copy_on(engine, y_round[step % Y_STAGE_TILES][:, first_tile:end_tile, :, :, :], in_)
+
+        def y_pairs(step):
+            return y_round[step % Y_STAGE_TILES][:].rearrange("j a u p e -> j (a u p e)").bitcast(F32)
 
         def turn_y(step):
-            words = y_round[step % 3][:].rearrange("j a u p e -> j (a u p e)").bitcast(F32)
-            for a in range(2):
-                for u in range(2):
-                    start = (2 * a + u) * P
-                    nc.tensor.transpose(word_view(word_bank[step % 2])[:, a, u, :], words[:, start : start + P], ident[:])
+            for quarter in range(4):
+                transpose_into(pair_bank[step % 2], quarter, y_pairs(step)[:, quarter * P : (quarter + 1) * P])
 
-        def quantize_y(step):
-            unit, piece = divmod(step, STEPS_PER_UNIT)
-            quantize(y_codes[unit % 2], y_scales[unit % 2], piece, y_packed[step % 3][:].bitcast(BF16))
+        def pack_y(step):
+            pack_pairs("scalar", y_packed[step % Y_STAGE_TILES][:], pair_bank[step % 2], 2)
 
-        def store_planes(step):
+        def turn_and_pack_last_y(engine, a):
+            for u in range(2):
+                transpose_into(act_bank[a], u, y_pairs(LAST)[:, (2 * a + u) * P : (2 * a + u + 1) * P])
+            pack_pairs(engine, y_packed[LAST % Y_STAGE_TILES][:, a * PIECE : (a + 1) * PIECE], act_bank[a], 1)
+
+        def quantize_and_store_planes(step):
             unit, piece = divmod(step, STEPS_PER_UNIT)
             fg, b = divmod(unit, B)
-            count = 1 if step >= STEPS - 2 else 2
-            if count == 1 or piece % 2 == 1:
-                lo, hi = (piece + 1 - count) * PIECE, (piece + 1) * PIECE
+            codes, scales = y_codes[unit % PLANE_UNITS], y_scales[unit % PLANE_UNITS]
+            quantize(codes, scales, piece * PIECE, y_packed[step % Y_STAGE_TILES][:].bitcast(BF16))
+            pieces = 1 if step >= STEPS - 2 else 2
+            if (piece + 1) % pieces == 0:
+                lo, hi = (piece + 1 - pieces) * PIECE, (piece + 1) * PIECE
                 words = out_1[fg].rearrange("p m t -> p (m t)").bitcast(I32)
-                nc.sync.dma_start(out=words[:, b * S + lo : b * S + hi], in_=y_codes[unit % 2][:, lo:hi].bitcast(I32))
+                nc.sync.dma_start(out=words[:, b * S + lo : b * S + hi], in_=codes[:, lo:hi].bitcast(I32))
             if piece == STEPS_PER_UNIT - 1:
                 rows = out_2[fg].bitcast(I32)
                 for q in range(4):
-                    queue = nc.scalar if unit == UNITS - 1 and q % 2 == 1 else nc.sync
+                    queue = nc.scalar if step == LAST and q % 2 == 1 else nc.sync
                     queue.dma_start(
                         out=rows[4 * q : 4 * q + 4, b * S // 4 : (b + 1) * S // 4],
-                        in_=y_scales[unit % 2][32 * q : 32 * q + 4, :].bitcast(I32),
+                        in_=scales[32 * q : 32 * q + 4, :].bitcast(I32),
                     )
 
-        load_x(0, 0)
-        load_x(0, 1)
+
+        load_x(0)
+        load_x(1)
         nc.sync.dma_start(out=b_raw[:], in_=b1.rearrange("(r c) -> r c", c=P))
         load_w1(0)
-        nc.sync.dma_start(out=tok_sb[:], in_=tok.rearrange("(g p t) -> p g t", g=S_GROUPS, t=PACK))
-        load_x(1, 0)
-        load_x(1, 1)
-        load_w2(0, 0)
-        load_w2(0, 1)
-        load_x(2, 0)
-        load_x(2, 1)
-        load_w2(1, 0)
-        load_w2(1, 1)
-        load_x(3, 0)
-        load_x(3, 1)
-        load_res(0)
-        load_w1(1)
-        load_res(1)
-        load_w1(2)
+        nc.sync.dma_start(out=tok_raw[:], in_=tok.rearrange("(g p t) -> p g t", g=S_GROUPS, t=PACK))
+        for side in range(2):
+            load_x(2 + 2 * side)
+            load_x(3 + 2 * side)
+            for g in range(S_GROUPS):
+                load_w2(g, side)
+        load_x(6)
+        load_x(7)
+        for unit in range(B):
+            load_res(unit)
+            load_w1(unit + 1)
 
         make_identity(nc, ident[:])
         nc.scalar.activation(out=b_rows[:], in_=ident[:], func=GELU)
 
-        turn_x(0, word_bank[0])
-        turn_x(1, word_bank[1])
-        copy_words(x_packed[0], word_bank[0], False)
-        nc.scalar.copy(out=b_rows[0 : F // P, :], in_=b_raw[:])
-        copy_words(x_packed[1], word_bank[1], False)
-        nc.tensor.transpose(a_bank[0][:, 0:P], b_rows[:], ident[:])
-        turn_x(2, word_bank[0])
-        copy_words(x_packed[2], word_bank[0], False)
-        if 0 == 0:
-            turn_x(3, word_bank[1])
-            copy_words(x_packed[3], word_bank[1], False)
-        pack_w(0, "vector")
+        turn_x(0, pair_bank[0])
+        turn_x(1, pair_bank[1])
+        pack_x(0, pair_bank[0])
+        nc.scalar.copy(out=b_rows[0:F_TILES, :], in_=b_raw[:])
+        pack_x(1, pair_bank[1])
+        transpose_into(act_bank[0], 0, b_rows[:])
+        for g in range(S_GROUPS):
+            widen_tok(g)
+            turn_x(2 + g, pair_bank[g])
+            pack_x(2 + g, pair_bank[g])
+        pack_w("vector", w_packed[0], w1_raw[0], 0)
         quantize_x(0)
-        quantize_w(0)
+        quantize(w1_codes[0], w1_scales[0], 0, flat(w_packed[0][:]))
         quantize_x(1)
-        nc.vector.tensor_copy(out=b_cols[:], in_=a_bank[0][:, 0 : F // P])
-        pack_w(1, "vector")
-        for i in range(2):
-            z_matmul(0, i)
-        quantize_w(1)
+        nc.vector.tensor_copy(out=b_cols[:], in_=act_bank[0][:, 0:F_TILES])
+        pack_w("vector", w_packed[1], w1_raw[0], PIECE)
+        z_matmuls(0)
+        quantize(w1_codes[0], w1_scales[0], PIECE, flat(w_packed[1][:]))
+        nc.vector.tensor_copy(out=tok_f32[:], in_=tok_raw[:].rearrange("p g t -> p (g t)"))
 
-        vector_packs = {0: [6], 1: [7], 2: [9], 3: [11]}
-        scalar_packs = {1: [8], 3: [10], 5: [12], 6: [13]}
-        x_half_at = {1: 4, 2: 5, 3: 6, 4: 7}
+        vector_w2 = dict(enumerate([(0, 0)] + [(1, piece) for piece in range(W1_FIRST_PASS - 1)]))
+        scalar_w2 = dict([(2 * piece - 1, (0, piece)) for piece in range(1, 4)] + [(LAG, (1, 3))])
+
+        def w2_stage_tile(g, piece):
+            last_on_vector = (g, piece) == vector_w2[W1_FIRST_PASS - 1]
+            return w_handover if last_on_vector else w_packed[(2 + 2 * piece + g) % W_PACKED_TILES]
 
         def live(step):
             return 0 <= step < STEPS
 
-        def mix_at(n):
-            c = n - LAG
-            if c < 30:
-                return [c] if live(c) else []
-            if c == 30:
-                return [c, c + 1]
-            return [c + 1] if c + 1 < STEPS else []
-
-        def finish_tile(a):
-            step = STEPS - 1
-            unit, piece = divmod(step, STEPS_PER_UNIT)
-            bank = a_bank[a]
-            words = y_round[step % 3][:].rearrange("j a u p e -> j (a u p e)").bitcast(F32)
-            for u in range(2):
-                start = (2 * a + u) * P
-                nc.tensor.transpose(bank[:, u * P : (u + 1) * P], words[:, start : start + P], ident[:])
-            packed = y_packed[step % 3][:, a * PIECE : (a + 1) * PIECE]
-            out = packed.rearrange("p (j u) -> p j u", u=2)
-            in_ = bank[:, 0 : 2 * P].rearrange("p (u j) -> p j u", u=2)
-            if a == 0:
-                nc.scalar.copy(out=out, in_=in_)
-            else:
-                nc.vector.tensor_copy(out=out, in_=in_)
-
         for n in range(STEPS + LAG + 1):
             c = n - LAG
-            if n % STEPS_PER_UNIT == 1 and 2 <= n // STEPS_PER_UNIT < UNITS:
+            x_half = n + 3 if 1 <= n <= 4 else None
+            w1_half = n - W1_FIRST_PASS
+            if n % STEPS_PER_UNIT == 1 and B <= n // STEPS_PER_UNIT < UNITS:
                 load_res(n // STEPS_PER_UNIT)
-            if n >= 40 and live(c - 2):
-                turn_y(c - 2)
-                copy_words(y_packed[(c - 2) % 3], word_bank[c % 2], False)
-            if live(c - 1) and c - 1 < 22:
-                round_y(c - 1, 0, 2, False)
-            for early in mix_at(n):
-                for i in range(2):
-                    mix_matmul(early, i)
-            for i in range(2):
-                if live(n) and n >= 2:
-                    z_matmul(n, i)
-                if n == 0:
-                    z_matmul(1, i)
+            if live(c - 1) and c - 1 < SPLIT_ROUND_FIRST:
+                round_y("scalar", c - 1, 0, 2)
+            if live(c):
+                mix_matmuls(c)
+            if n == 0:
+                z_matmuls(1)
+            if live(n) and n >= 2:
+                z_matmuls(n)
+
             if live(c):
                 add_res(c, 0)
-                if n >= 14 and live(n - 2):
+                if n > LAST and live(n - 2):
                     quantize_h(n - 2)
-                if c >= 22:
-                    round_y(c, 0, 1, False)
+                if c >= SPLIT_ROUND_FIRST:
+                    round_y("scalar", c, 0, 1)
                 add_res(c, 1)
                 store_y(c)
-            for wp in vector_packs.get(n - 1, []):
-                if slot_of[wp] != 4:
-                    quantize_w(wp)
+            if n - 1 in vector_w2 and w1_half < 0:
+                quantize_w2(*vector_w2[n - 1])
             if n == 0:
                 quantize_x(2)
-            if n == 0:
                 quantize_x(3)
-            for xh in dict({2: [4], 3: [5], 4: [6], 5: [7]}).get(n, []):
-                quantize_x(xh)
-            if live(n - 2) and n < 14:
+            if 2 <= n <= 5:
+                quantize_x(n + 2)
+            if live(n - 2) and n < PAIRS_FIRST:
                 quantize_h(n - 2)
             if live(c - 3):
-                quantize_y(c - 3)
-                store_planes(c - 3)
-            for wp in scalar_packs.get(n - 2, []):
-                quantize_w(wp)
-            if live(c) and c >= 22:
-                round_y(c, 1, 2, True)
-            for wp in vector_packs.get(n, []):
-                pack_w(wp, "vector")
-            if 0 <= n - 4 < len(chain):
-                quantize_w(*chain[n - 4])
-            if 0 <= n - 4 < len(chain) - 1:
-                pack_w(chain[n - 4 + 1][0], "gpsimd", chain[n - 4 + 1][1], chain[n - 4 + 1][2])
-            for i in range(2):
-                if live(n):
+                quantize_and_store_planes(c - 3)
+            if n - 2 in scalar_w2:
+                quantize_w2(*scalar_w2[n - 2])
+            if live(c) and c >= SPLIT_ROUND_FIRST:
+                round_y("vector", c, 1, 2)
+            if n in vector_w2:
+                pack_w2("vector", *vector_w2[n], w2_stage_tile(*vector_w2[n]))
+            if w1_half == 0:
+                quantize_w2(*vector_w2[n - 1])
+            if 1 <= w1_half <= W1_HALVES:
+                quantize_w1_half(w1_half - 1)
+            if PAIRS_FIRST <= n <= LAST:
+                quantize_h(n - 2)
+            if 0 <= w1_half < W1_HALVES:
+                pack_w1_half(w1_half)
+
+            if live(n):
+                for i in tile_order(n):
                     gelu(n, i)
-            if n == 0 and 0 == 1:
-                turn_x(3, word_bank[1])
-                copy_words(x_packed[3], word_bank[1], True)
+                if as_pairs(n, 1):
+                    scale_rows(n)
+
             if live(n - 1):
                 turn_act(n - 1, 0)
-            if live(c - 2) and n < 40:
+            if live(c - 2):
                 turn_y(c - 2)
             if live(n - 1):
                 turn_act(n - 1, 1)
-            if n in x_half_at:
-                turn_x(x_half_at[n], word_bank[n % 2])
-            for i in range(2):
-                if live(n - 1):
-                    scale_tokens(n - 1, i)
-            if live(c - 2) and n < 40:
-                copy_words(y_packed[(c - 2) % 3], word_bank[c % 2], False)
-            if n in x_half_at:
-                copy_words(x_packed[x_half_at[n] % 4], word_bank[n % 2], False)
-            for wp in scalar_packs.get(n, []):
-                pack_w(wp, "scalar")
-        finish_tile(0)
-        quantize_y(STEPS - 2)
-        store_planes(STEPS - 2)
-        finish_tile(1)
-        quantize_y(STEPS - 1)
-        store_planes(STEPS - 1)
+            if x_half is not None:
+                turn_x(x_half, pair_bank[n % 2])
+            if 5 <= n < 5 + S_GROUPS:
+                spread_tok(n - 5, pair_bank[n % 2])
+
+            if live(n - 1):
+                pack_h(n - 1, 0)
+                pack_h(n - 1, 1)
+            if live(c - 2):
+                pack_y(c - 2)
+            if x_half is not None:
+                pack_x(x_half, pair_bank[n % 2])
+            if n in scalar_w2:
+                pack_w2("scalar", *scalar_w2[n], w2_stage_tile(*scalar_w2[n]))
+
+        turn_and_pack_last_y("scalar", 0)
+        quantize_and_store_planes(LAST - 1)
+        turn_and_pack_last_y("vector", 1)
+        quantize_and_store_planes(LAST)

from contextlib import ExitStack

import concourse.mybir as mybir
from concourse.masks import make_identity

B, S, D, F = 2, 1024, 512, 1536
FLOPS = 2 * B * S * D * F + 2 * B * S * S * F

F32 = mybir.dt.float32
BF16 = mybir.dt.bfloat16
I32 = mybir.dt.int32
U32 = mybir.dt.uint32
U8 = mybir.dt.uint8
FP8X4 = mybir.dt.float8_e4m3fn_x4
GELU = mybir.ActivationFunctionType.Gelu_apprx_tanh
ADD = mybir.AluOpType.add
MULT = mybir.AluOpType.mult

P = 128
PACK = 4
GROUP = P * PACK
PIECE = 2 * P
HALF = PIECE // 2
F_GROUPS = F // GROUP
S_GROUPS = S // GROUP
F_TILES = F // P
STEPS_PER_UNIT = 4
UNITS = F_GROUPS * B
STEPS = UNITS * STEPS_PER_UNIT
LAST = STEPS - 1
LAG = STEPS_PER_UNIT + 2

W1_FIRST_PASS = 4
W1_HALVES = (F_GROUPS - 1) * GROUP // HALF
PAIRS_FIRST = W1_FIRST_PASS + W1_HALVES
SPLIT_ROUND_FIRST = STEPS - 2

RES_TILES = 3
W_PACKED_TILES = 4
X_PACKED_TILES = 4
ACT_STEPS = 3
H_PACKED_TILES = 5
H_UNITS = 3
Y_TILES = 4
Y_STAGE_TILES = 3
PLANE_UNITS = 2


def tile_gelu_token_mix_residual_h3_kernel(tc, x, w1, b1, tok, w2, res, out_0, out_1, out_2):
    nc = tc.nc
    with ExitStack() as ctx:
        sbuf = ctx.enter_context(tc.tile_pool(name="sbuf", bufs=1))
        psum = ctx.enter_context(tc.psum_pool(name="psum", bufs=1))
        ctx.enter_context(tc.manual_schedule())

        def tiles(name, count, shape, dtype):
            return [sbuf.tile(shape, dtype, name="%s%d" % (name, n), align_bytes=64) for n in range(count)]

        def banks(name):
            return [psum.tile([P, GROUP], F32, name="%s%d" % (name, i)) for i in range(2)]

        z_bank = banks("z_bank")
        act_bank = banks("act_bank")
        mix_bank = banks("mix_bank")
        pair_bank = banks("pair_bank")

        ident = sbuf.tile([P, P], F32, name="ident", align_bytes=64)
        b_raw = sbuf.tile([F_TILES, P], BF16, name="b_raw", align_bytes=64)
        b_rows = sbuf.tile([P, P], F32, name="b_rows", align_bytes=64)
        b_cols = sbuf.tile([P, F_TILES], F32, name="b_cols", align_bytes=64)
        tok_raw = sbuf.tile([P, S_GROUPS, PACK], BF16, name="tok_raw", align_bytes=64)
        tok_f32 = sbuf.tile([P, S_GROUPS * PACK], F32, name="tok_f32", align_bytes=64)
        tok_wide = tiles("tok_wide", S_GROUPS, [P, P // 2, PACK, 2], BF16)
        tok_rows = tiles("tok_rows", S_GROUPS, [P, GROUP], F32)

        x_raw = tiles("x_raw", B * S_GROUPS * 2, [P, 2, D], BF16)
        w1_raw = tiles("w1_raw", F_GROUPS, [P, PACK, GROUP], BF16)
        w2_raw = tiles("w2_raw", S_GROUPS * 2, [P, PACK, GROUP], BF16)
        res_sb = tiles("res_sb", RES_TILES, [P, S // P, GROUP], BF16)
        w_packed = tiles("w_packed", W_PACKED_TILES, [P, PIECE, PACK], BF16)
        w_handover = sbuf.tile([P, PIECE, PACK], BF16, name="w_handover", align_bytes=64)
        x_packed = tiles("x_packed", X_PACKED_TILES, [P, 2 * PIECE], F32)
        x_codes = tiles("x_codes", B * S_GROUPS, [P, GROUP], U32)
        x_scales = tiles("x_scales", B * S_GROUPS, [P, GROUP], U8)
        w1_codes = tiles("w1_codes", F_GROUPS, [P, GROUP], U32)
        w1_scales = tiles("w1_scales", F_GROUPS, [P, GROUP], U8)
        w2_codes = tiles("w2_codes", S_GROUPS, [P, S], U32)
        w2_scales = tiles("w2_scales", S_GROUPS, [P, S], U8)
        act = tiles("act", 2 * ACT_STEPS, [P, GROUP], F32)
        h_packed = tiles("h_packed", H_PACKED_TILES, [P, PIECE, PACK], BF16)
        h_codes = tiles("h_codes", H_UNITS * S_GROUPS, [P, GROUP], U32)
        h_scales = tiles("h_scales", H_UNITS * S_GROUPS, [P, GROUP], U8)
        y_sb = tiles("y_sb", Y_TILES, [P, 2, GROUP], F32)
        y_round = tiles("y_round", Y_STAGE_TILES, [P, 2, 2, P, 2], BF16)
        y_packed = tiles("y_packed", Y_STAGE_TILES, [P, 2 * PIECE], F32)
        y_codes = tiles("y_codes", PLANE_UNITS, [P, S], U32)
        y_scales = tiles("y_scales", PLANE_UNITS, [P, S], U8)

        def copy_on(engine, out, in_):
            if engine == "vector":
                nc.vector.tensor_copy(out=out, in_=in_)
            else:
                nc.scalar.copy(out=out, in_=in_)

        def flat(packed):
            return packed.rearrange("p c t -> p (c t)")

        def quantize(codes, scales, first_col, packed):
            cols = slice(first_col, first_col + packed.shape[1] // PACK)
            nc.vector.quantize_mx(out=codes[:, cols].bitcast(FP8X4), scales=scales[:, cols], in_=packed)

        def matmul(bank, l_codes, l_scales, l_tile, r_codes, r_scales, start, stop):
            cols = slice(l_tile * P, (l_tile + 1) * P)
            nc.tensor.matmul_mx(
                out=bank[:],
                lhsT=l_codes[:, cols].bitcast(FP8X4),
                lhsT_scale=l_scales[:, cols],
                rhs=r_codes[:].bitcast(FP8X4),
                rhs_scale=r_scales[:],
                start=start,
                stop=stop,
            )

        def transpose_into(bank, quarter, in_):
            nc.tensor.transpose(bank[:, quarter * P : (quarter + 1) * P], in_, ident[:])

        def pack_pairs(engine, out, bank, row_tiles):
            in_ = bank[:, 0 : row_tiles * PIECE].rearrange("p (a u j) -> p a j u", a=row_tiles, u=2)
            copy_on(engine, out.rearrange("p (a j u) -> p a j u", a=row_tiles, u=2), in_)


        def load_x(xh):
            b, g = divmod(xh // 2, S_GROUPS)
            rows = x[b, g * GROUP : (g + 1) * GROUP, :].rearrange("(p t) d -> p t d", t=PACK)
            nc.sync.dma_start(out=x_raw[xh][:], in_=rows[:, 2 * (xh % 2) : 2 * (xh % 2) + 2, :])

        def load_w1(fg):
            cols = w1[:, fg * GROUP : (fg + 1) * GROUP]
            nc.sync.dma_start(out=w1_raw[fg][:], in_=cols.rearrange("(p t) c -> p t c", t=PACK))

        def load_w2(g, side):
            rows = w2[g * GROUP : (g + 1) * GROUP, side * GROUP : (side + 1) * GROUP]
            nc.sync.dma_start(out=w2_raw[2 * g + side][:], in_=rows.rearrange("(p t) c -> p t c", t=PACK))

        def load_res(unit):
            fg, b = divmod(unit, B)
            cols = res[b, :, fg * GROUP : (fg + 1) * GROUP]
            nc.sync.dma_start(out=res_sb[unit % RES_TILES][:], in_=cols.rearrange("(a j) f -> j a f", j=P))


        def pack_w(engine, packed, raw, first_col):
            in_ = raw[:, :, first_col : first_col + PIECE].rearrange("p t (c i) -> p c t i", i=4)
            copy_on(engine, packed[:].rearrange("p (c i) t -> p c t i", i=4), in_)

        w2_stage = {}

        def pack_w2(engine, g, piece, packed):
            w2_stage[(g, piece)] = packed
            pack_w(engine, packed, w2_raw[2 * g + piece // 2], (piece % 2) * PIECE)

        def quantize_w2(g, piece):
            quantize(w2_codes[g], w2_scales[g], piece * PIECE, flat(w2_stage[(g, piece)][:]))

        def pack_w1_half(half):
            fg, col = divmod(GROUP + half * HALF, GROUP)
            in_ = w1_raw[fg][:, :, col : col + HALF].rearrange("p t c -> p c t")
            nc.gpsimd.tensor_scalar(out=w_handover[:, 0:HALF, :], in0=in_, scalar1=1.0, scalar2=0.0, op0=MULT, op1=ADD)

        def quantize_w1_half(half):
            fg, col = divmod(GROUP + half * HALF, GROUP)
            quantize(w1_codes[fg], w1_scales[fg], col, flat(w_handover[:, 0:HALF, :]))


        def turn_x(xh, bank):
            for a in range(2):
                pairs = x_raw[xh][:, a, :].bitcast(F32)
                for u in range(2):
                    transpose_into(bank, 2 * a + u, pairs[:, u : D // 2 : 2])

        def pack_x(xh, bank):
            pack_pairs("scalar", x_packed[xh % X_PACKED_TILES][:], bank, 2)

        def quantize_x(xh):
            packed = x_packed[xh % X_PACKED_TILES][:].bitcast(BF16)
            quantize(x_codes[xh // 2], x_scales[xh // 2], (xh % 2) * PIECE, packed)


        def widen_tok(g):
            in_ = tok_raw[:, g, :].unsqueeze(1).unsqueeze(3).to_broadcast([P, P // 2, PACK, 2])
            nc.scalar.copy(out=tok_wide[g][:], in_=in_)

        def spread_tok(g, bank):
            for t in range(PACK):
                transpose_into(bank, t, tok_f32[:, PACK * g + t : PACK * g + t + 1].to_broadcast([P, P]))
            nc.scalar.copy(
                out=tok_rows[g][:].rearrange("f (u p e) -> f u p e", u=2, e=2),
                in_=bank[:].rearrange("f (u e p) -> f u p e", u=2, e=2),
            )


        def first_parts(step):
            unit, rest = divmod(step, STEPS_PER_UNIT)
            fg, b = divmod(unit, B)
            g, piece = divmod(rest, 2)
            return unit, fg, b, g, piece

        def as_pairs(step, i):
            return i == 1 and PAIRS_FIRST <= step < LAST

        def tile_order(step):
            return [1, 0] if as_pairs(step, 1) else [0, 1]

        def z_of(step, i):
            return mix_bank[i] if step < LAG and step % 2 == 1 else z_bank[i]

        def act_of(step, i):
            return act[2 * (step % ACT_STEPS) + i]

        def z_matmuls(step):
            unit, fg, b, g, piece = first_parts(step)
            xg = b * S_GROUPS + g
            for i in tile_order(step):
                matmul(z_of(step, i), w1_codes[fg], w1_scales[fg], 2 * piece + i, x_codes[xg], x_scales[xg], True, True)

        def gelu(step, i):
            unit, fg, b, g, piece = first_parts(step)
            f_tile = PACK * fg + 2 * piece + i
            out, in_ = act_of(step, i)[:], z_of(step, i)[:]
            if as_pairs(step, i):
                out = out.rearrange("f (u p e) -> f u p e", u=2, e=2)
                in_ = in_.rearrange("f (u e p) -> f u p e", u=2, e=2)
            nc.scalar.activation(out=out, in_=in_, func=GELU, bias=b_cols[:, f_tile : f_tile + 1])

        def h_rows(step):
            return flat(h_packed[(step - 2) % H_PACKED_TILES][:])[:, 0:GROUP]

        def scale_rows(step):
            unit, fg, b, g, piece = first_parts(step)
            nc.gpsimd.tensor_tensor(out=h_rows(step), in0=act_of(step, 1)[:], in1=tok_rows[g][:], op=MULT)

        def turn_act(step, i):
            source = h_rows(step).bitcast(F32) if as_pairs(step, i) else act_of(step, i)[:]
            for quarter in range(source.shape[1] // P):
                transpose_into(act_bank[i], quarter, source[:, quarter * P : (quarter + 1) * P])

        def pack_h(step, i):
            unit, fg, b, g, piece = first_parts(step)
            packed = h_packed[step % H_PACKED_TILES][:, i * P : (i + 1) * P, :]
            if as_pairs(step, i):
                pack_pairs("vector", flat(packed).bitcast(F32), act_bank[i], 1)
            else:
                nc.vector.tensor_tensor(
                    out=packed.rearrange("p (c e) t -> p c t e", e=2),
                    in0=act_bank[i][:].rearrange("p (t c e) -> p c t e", t=PACK, e=2),
                    in1=tok_wide[g][:],
                    op=MULT,
                )

        def quantize_h(step):
            unit, fg, b, g, piece = first_parts(step)
            hg = (unit % H_UNITS) * S_GROUPS + g
            quantize(h_codes[hg], h_scales[hg], piece * PIECE, flat(h_packed[step % H_PACKED_TILES][:]))


        def mix_of(step, i):
            return z_bank[i] if step + LAG > STEPS and step % 2 == 1 else mix_bank[i]

        def mix_matmuls(step):
            unit, piece = divmod(step, STEPS_PER_UNIT)
            for i in range(2):
                for g in range(S_GROUPS):
                    hg = (unit % H_UNITS) * S_GROUPS + g
                    matmul(
                        mix_of(step, i), w2_codes[g], w2_scales[g], 2 * piece + i, h_codes[hg], h_scales[hg],
                        g == 0, g == S_GROUPS - 1,
                    )

        def add_res(step, i):
            unit, piece = divmod(step, STEPS_PER_UNIT)
            nc.vector.tensor_tensor(
                out=y_sb[step % Y_TILES][:, i, :],
                in0=mix_of(step, i)[:],
                in1=res_sb[unit % RES_TILES][:, 2 * piece + i, :],
                op=ADD,
            )

        def store_y(step):
            unit, piece = divmod(step, STEPS_PER_UNIT)
            fg, b = divmod(unit, B)
            rows = out_0[b, piece * PIECE : (piece + 1) * PIECE, fg * GROUP : (fg + 1) * GROUP]
            nc.sync.dma_start(out=rows.rearrange("(a j) f -> j a f", j=P), in_=y_sb[step % Y_TILES][:])

        def round_y(engine, step, first_tile, end_tile):
            in_ = y_sb[step % Y_TILES][:, first_tile:end_tile, :].rearrange("j a (p u e) -> j a u p e", u=2, e=2)
            copy_on(engine, y_round[step % Y_STAGE_TILES][:, first_tile:end_tile, :, :, :], in_)

        def y_pairs(step):
            return y_round[step % Y_STAGE_TILES][:].rearrange("j a u p e -> j (a u p e)").bitcast(F32)

        def turn_y(step):
            for quarter in range(4):
                transpose_into(pair_bank[step % 2], quarter, y_pairs(step)[:, quarter * P : (quarter + 1) * P])

        def pack_y(step):
            pack_pairs("scalar", y_packed[step % Y_STAGE_TILES][:], pair_bank[step % 2], 2)

        def turn_and_pack_last_y(engine, a):
            for u in range(2):
                transpose_into(act_bank[a], u, y_pairs(LAST)[:, (2 * a + u) * P : (2 * a + u + 1) * P])
            pack_pairs(engine, y_packed[LAST % Y_STAGE_TILES][:, a * PIECE : (a + 1) * PIECE], act_bank[a], 1)

        def quantize_and_store_planes(step):
            unit, piece = divmod(step, STEPS_PER_UNIT)
            fg, b = divmod(unit, B)
            codes, scales = y_codes[unit % PLANE_UNITS], y_scales[unit % PLANE_UNITS]
            quantize(codes, scales, piece * PIECE, y_packed[step % Y_STAGE_TILES][:].bitcast(BF16))
            pieces = 1 if step >= STEPS - 2 else 2
            if (piece + 1) % pieces == 0:
                lo, hi = (piece + 1 - pieces) * PIECE, (piece + 1) * PIECE
                words = out_1[fg].rearrange("p m t -> p (m t)").bitcast(I32)
                nc.sync.dma_start(out=words[:, b * S + lo : b * S + hi], in_=codes[:, lo:hi].bitcast(I32))
            if piece == STEPS_PER_UNIT - 1:
                rows = out_2[fg].bitcast(I32)
                for q in range(4):
                    queue = nc.scalar if step == LAST and q % 2 == 1 else nc.sync
                    queue.dma_start(
                        out=rows[4 * q : 4 * q + 4, b * S // 4 : (b + 1) * S // 4],
                        in_=scales[32 * q : 32 * q + 4, :].bitcast(I32),
                    )


        load_x(0)
        load_x(1)
        nc.sync.dma_start(out=b_raw[:], in_=b1.rearrange("(r c) -> r c", c=P))
        load_w1(0)
        nc.sync.dma_start(out=tok_raw[:], in_=tok.rearrange("(g p t) -> p g t", g=S_GROUPS, t=PACK))
        for side in range(2):
            load_x(2 + 2 * side)
            load_x(3 + 2 * side)
            for g in range(S_GROUPS):
                load_w2(g, side)
        load_x(6)
        load_x(7)
        for unit in range(B):
            load_res(unit)
            load_w1(unit + 1)

        make_identity(nc, ident[:])
        nc.scalar.activation(out=b_rows[:], in_=ident[:], func=GELU)

        turn_x(0, pair_bank[0])
        turn_x(1, pair_bank[1])
        pack_x(0, pair_bank[0])
        nc.scalar.copy(out=b_rows[0:F_TILES, :], in_=b_raw[:])
        pack_x(1, pair_bank[1])
        transpose_into(act_bank[0], 0, b_rows[:])
        for g in range(S_GROUPS):
            widen_tok(g)
            turn_x(2 + g, pair_bank[g])
            pack_x(2 + g, pair_bank[g])
        pack_w("vector", w_packed[0], w1_raw[0], 0)
        quantize_x(0)
        quantize(w1_codes[0], w1_scales[0], 0, flat(w_packed[0][:]))
        quantize_x(1)
        nc.vector.tensor_copy(out=b_cols[:], in_=act_bank[0][:, 0:F_TILES])
        pack_w("vector", w_packed[1], w1_raw[0], PIECE)
        z_matmuls(0)
        quantize(w1_codes[0], w1_scales[0], PIECE, flat(w_packed[1][:]))
        nc.vector.tensor_copy(out=tok_f32[:], in_=tok_raw[:].rearrange("p g t -> p (g t)"))

        vector_w2 = dict(enumerate([(0, 0)] + [(1, piece) for piece in range(W1_FIRST_PASS - 1)]))
        scalar_w2 = dict([(2 * piece - 1, (0, piece)) for piece in range(1, 4)] + [(LAG, (1, 3))])

        def w2_stage_tile(g, piece):
            last_on_vector = (g, piece) == vector_w2[W1_FIRST_PASS - 1]
            return w_handover if last_on_vector else w_packed[(2 + 2 * piece + g) % W_PACKED_TILES]

        def live(step):
            return 0 <= step < STEPS

        for n in range(STEPS + LAG + 1):
            c = n - LAG
            x_half = n + 3 if 1 <= n <= 4 else None
            w1_half = n - W1_FIRST_PASS
            if n % STEPS_PER_UNIT == 1 and B <= n // STEPS_PER_UNIT < UNITS:
                load_res(n // STEPS_PER_UNIT)
            if live(c - 1) and c - 1 < SPLIT_ROUND_FIRST:
                round_y("scalar", c - 1, 0, 2)
            if live(c):
                mix_matmuls(c)
            if n == 0:
                z_matmuls(1)
            if live(n) and n >= 2:
                z_matmuls(n)

            if live(c):
                add_res(c, 0)
                if n > LAST and live(n - 2):
                    quantize_h(n - 2)
                if c >= SPLIT_ROUND_FIRST:
                    round_y("scalar", c, 0, 1)
                add_res(c, 1)
                store_y(c)
            if n - 1 in vector_w2 and w1_half < 0:
                quantize_w2(*vector_w2[n - 1])
            if n == 0:
                quantize_x(2)
                quantize_x(3)
            if 2 <= n <= 5:
                quantize_x(n + 2)
            if live(n - 2) and n < PAIRS_FIRST:
                quantize_h(n - 2)
            if live(c - 3):
                quantize_and_store_planes(c - 3)
            if n - 2 in scalar_w2:
                quantize_w2(*scalar_w2[n - 2])
            if live(c) and c >= SPLIT_ROUND_FIRST:
                round_y("vector", c, 1, 2)
            if n in vector_w2:
                pack_w2("vector", *vector_w2[n], w2_stage_tile(*vector_w2[n]))
            if w1_half == 0:
                quantize_w2(*vector_w2[n - 1])
            if 1 <= w1_half <= W1_HALVES:
                quantize_w1_half(w1_half - 1)
            if PAIRS_FIRST <= n <= LAST:
                quantize_h(n - 2)
            if 0 <= w1_half < W1_HALVES:
                pack_w1_half(w1_half)

            if live(n):
                for i in tile_order(n):
                    gelu(n, i)
                if as_pairs(n, 1):
                    scale_rows(n)

            if live(n - 1):
                turn_act(n - 1, 0)
            if live(c - 2):
                turn_y(c - 2)
            if live(n - 1):
                turn_act(n - 1, 1)
            if x_half is not None:
                turn_x(x_half, pair_bank[n % 2])
            if 5 <= n < 5 + S_GROUPS:
                spread_tok(n - 5, pair_bank[n % 2])

            if live(n - 1):
                pack_h(n - 1, 0)
                pack_h(n - 1, 1)
            if live(c - 2):
                pack_y(c - 2)
            if x_half is not None:
                pack_x(x_half, pair_bank[n % 2])
            if n in scalar_w2:
                pack_w2("scalar", *scalar_w2[n], w2_stage_tile(*scalar_w2[n]))

        turn_and_pack_last_y("scalar", 0)
        quantize_and_store_planes(LAST - 1)
        turn_and_pack_last_y("vector", 1)
        quantize_and_store_planes(LAST)
